import numpy as np
import ml_dtypes


def mxq(x, axis, fmt="e4m3"):
    dtype, down = {"e4m3": (ml_dtypes.float8_e4m3fn, 7), "e5m2": (ml_dtypes.float8_e5m2, 14)}[fmt]
    v = np.moveaxis(np.asarray(x, np.float32).astype(ml_dtypes.bfloat16).astype(np.float64), axis, -1)
    blocks = v.reshape(v.shape[:-1] + (-1, 32))
    amax = np.abs(blocks).max(-1, keepdims=True)
    byte = np.maximum(np.where(amax > 0, np.frexp(amax)[1] - 1 + 127, 0) - down, 1)
    scale = np.exp2(byte - 127.0)
    codes = (blocks / scale).astype(np.float32).astype(dtype).astype(np.float64)
    return np.moveaxis((codes * scale).reshape(v.shape), -1, axis)


WIDE = False


def mx_kscale(k):
    if not WIDE:
        return np.ones(k)
    levels = np.array([10, -10, 5, -5, 0])
    if k % 512:
        return np.exp2(np.random.permutation(np.resize(levels, k // 32))).repeat(32)
    a = np.empty((k // 512, 16))
    for p in range(k // 512):
        a[p, :8] = np.random.permutation(np.resize(levels, 8))
        for g in range(8):
            far = levels[np.abs(levels - a[p, g]) >= 10]
            a[p, g + 8] = far[np.random.randint(len(far))]
    return np.exp2(a.ravel()).repeat(32)


def f64(x):
    return np.asarray(x).astype(np.float64)


def striped(idx):
    return np.tile(idx.reshape(-1, 16).T, (8, 1)).astype(np.uint16)


def unstriped(offs):
    return offs[:16].T.reshape(-1).astype(np.int64)


E2M1 = np.array([0.0, 0.5, 1.0, 1.5, 2.0, 3.0, 4.0, 6.0, -0.0, -0.5, -1.0, -1.5, -2.0, -3.0, -4.0, -6.0])


def pack_weight(w, fmt):
    k, n = w.shape
    w = f64(np.asarray(w, np.float32).astype(ml_dtypes.bfloat16)).reshape(k // 32, 32, n)
    amax = np.abs(w).max(1)
    if fmt == "e4m3":
        byte = np.frexp(amax)[1] - 1 + 127 - 7
    else:
        mant, ex = np.frexp(amax / 6.0)
        byte = np.where(mant > 0.5, ex, ex - 1) + 127
    byte = np.clip(np.where(amax > 0, byte, 1), 1, 254)
    scaled = (w * np.exp2(127.0 - byte)[:, None, :]).reshape(k, n).astype(np.float32)
    by_word = np.ascontiguousarray(scaled.reshape(k // 512, 128, 4, n).transpose(0, 1, 3, 2))
    if fmt == "e4m3":
        words = by_word.astype(ml_dtypes.float8_e4m3fn).view(np.uint8)
    else:
        c = by_word.astype(ml_dtypes.float4_e2m1fn).view(np.uint8) & 0xF
        words = (c[..., 0::2] | (c[..., 1::2] << 4)).reshape(k // 512, 128, 2 * n)
    return np.ascontiguousarray(words), np.ascontiguousarray(byte.astype(np.uint8).reshape(k // 512, 16, n))


def unpack_weight(words, scales, fmt):
    g, _, n = scales.shape
    words = np.ascontiguousarray(words).reshape(g, 128, n, -1)
    if fmt == "e4m3":
        vals = words.view(ml_dtypes.float8_e4m3fn).astype(np.float64)
    else:
        nib = np.empty((g, 128, n, 4), np.uint8)
        nib[..., 0::2] = words & 0xF
        nib[..., 1::2] = words >> 4
        vals = E2M1[nib]
    vals = vals * np.repeat(np.exp2(scales.astype(np.float64) - 127.0), 8, axis=1)[..., None]
    return vals.transpose(0, 1, 3, 2).reshape(g * 512, n)


def gelu(v):
    return 0.5 * v * (1.0 + np.tanh(np.sqrt(2.0 / np.pi) * (v + 0.044715 * v**3)))


K, K2, H, N, T, S = 1024, 512, 1024, 384, 2048, 1024

def setup_inputs():
    n = np.random.standard_normal
    s = mx_kscale(K)[:, None]
    s2 = mx_kscale(K2)[:, None]
    u = mx_kscale(H)[:, None]
    d = {}
    d["tab_words"], d["tab_scales"] = pack_weight(n((K, T)) * s, "e4m3")
    d["offs"] = striped(np.random.permutation(T)[:S])
    d["xs_words"], d["xs_scales"] = pack_weight(n((K2, S)) * s2, "e4m3")
    d["w1"] = (n((K, H)) / K**0.5 / s * u.T).astype(np.float32)
    d["b1"] = (0.5 * n(H) * u[:, 0]).astype(np.float32)
    d["w2_words"], d["w2_scales"] = pack_weight(n((K2, H)) / K2**0.5 / s2 * u.T, "e4m3")
    d["w3"] = (n((H, N)) / H**0.5 / u).astype(np.float32)
    d["w4_words"], d["w4_scales"] = pack_weight(0.7 * n((H, N)) / H**0.5 / u, "e2m1")
    d["swing"] = np.random.uniform(1.6, 2.8, N).astype(np.float32)
    return d

def reference(tab_words, tab_scales, offs, xs_words, xs_scales, w1, b1, w2_words, w2_scales, w3, w4_words, w4_scales, swing):
    v = unpack_weight(tab_words, tab_scales, "e4m3")[:, unstriped(offs)]
    xs = unpack_weight(xs_words, xs_scales, "e4m3")
    w2 = unpack_weight(w2_words, w2_scales, "e4m3")
    w4 = unpack_weight(w4_words, w4_scales, "e2m1")
    soil = (mxq(f64(w1), 0, "e4m3").T @ v) + f64(b1)[:, None]
    motor = w2.T @ xs
    top = mxq(np.maximum(soil, motor), 0, "e4m3")
    gap = mxq(soil - motor, 0, "e4m3")
    y1 = mxq(f64(w3), 0, "e4m3").T @ top
    y2 = w4.T @ gap
    angle = f64(swing)[:, None] * np.tanh(y2)
    return y1 - np.cos(angle)

@@ -1,0 +1,332 @@
+import math
+from contextlib import ExitStack
+
+import concourse.mybir as mybir
+
+K, K2, H, N, T, S = 1024, 512, 1024, 384, 2048, 1024
+FLOPS = 2 * S * (K * H + K2 * H + 2 * H * N)
+
+F32 = mybir.dt.float32
+BF16 = mybir.dt.bfloat16
+I32 = mybir.dt.int32
+U32 = mybir.dt.uint32
+U16 = mybir.dt.uint16
+U8 = mybir.dt.uint8
+FP8X4 = mybir.dt.float8_e4m3fn_x4
+FP4X4 = mybir.dt.float4_e2m1fn_x4
+ACT = mybir.ActivationFunctionType
+ALU = mybir.AluOpType
+
+P = 128
+PASS = 512
+GATHER = 512
+CHUNK = 256
+N_TILES = N // P
+
+
+def tile_list_wheel_slip_features_kernel(
+    tc, tab_words, tab_scales, offs, xs_words, xs_scales, w1, b1, w2_words, w2_scales, w3, w4_words, w4_scales, swing, out
+):
+    nc = tc.nc
+    with ExitStack() as ctx:
+        keep = ctx.enter_context(tc.tile_pool(name="keep", bufs=1))
+        ring = ctx.enter_context(tc.tile_pool(name="ring", bufs=3))
+        psum = ctx.enter_context(tc.psum_pool(name="psum", bufs=1))
+
+        def held(name, shape, dtype):
+            return keep.tile(shape, dtype, name=name, align_bytes=64)
+
+        offsets = keep.tile([P, S // 16], U16, name="offsets")
+        nc.sync.dma_start(offsets[:], offs)
+
+        tab_s = held("tab_s", [P, T], U8)
+        nc.vector.memset(tab_s[:].bitcast(I32), 0)
+        w2_sraw = held("w2_sraw", [P, PASS], U8)
+        nc.vector.memset(w2_sraw[:].bitcast(I32), 0)
+        warm = held("warm", [P, 2], F32)
+        nc.vector.memset(warm[:, 0:1], 0.0)
+        nc.scalar.activation(warm[:, 1:2], warm[:, 0:1], ACT.Silu)
+
+        xs_s = held("xs_s", [P, S], U8)
+        nc.vector.memset(xs_s[:].bitcast(I32), 0)
+        w4_s = held("w4_s", [P, 2, N], U8)
+        nc.vector.memset(w4_s[:].rearrange("p a c -> p (a c)").bitcast(I32), 0)
+
+        def load_words(name, src):
+            width = src.shape[1]
+            dst = held(name, [P, width], I32)
+            nc.sync.dma_start(dst[:], src.rearrange("p c i -> p (c i)").bitcast(I32))
+            return dst
+
+        w1_raw = {}
+
+        def load_w1(a, b, h):
+            dst = held("w1_raw%d%d%d" % (a, b, h), [P, 4, 256], F32)
+            cols = slice(PASS * b + 256 * h, PASS * b + 256 * (h + 1))
+            nc.sync.dma_start(dst[:], w1[PASS * a : PASS * (a + 1), cols].rearrange("(p j) c -> p j c", j=4))
+            w1_raw[a, b, h] = dst
+
+        w2_raw = [load_words("w2_raw0", w2_words[0][:, 0:PASS, :])]
+        load_w1(0, 0, 0)
+        for q in range(4):
+            nc.sync.dma_start(tab_s[32 * q : 32 * q + 8, :].bitcast(I32), tab_scales[:, 4 * q : 4 * q + 4, :].bitcast(I32))
+        load_w1(0, 0, 1)
+        tab_w = [load_words("tab_w0", tab_words[0])]
+        for q in range(4):
+            nc.sync.dma_start(
+                w2_sraw[32 * q : 32 * q + 8, :].bitcast(I32),
+                w2_scales[0, 4 * q : 4 * q + 4, :].rearrange("r (b c) -> b r c", b=2).bitcast(I32),
+            )
+        load_w1(1, 0, 0)
+        load_w1(1, 0, 1)
+        tab_w.append(load_words("tab_w1", tab_words[1]))
+        bias = held("bias", [P, 2, 4], F32)
+        nc.sync.dma_start(bias[:], b1.rearrange("(b p t) -> p b t", b=2, t=4))
+        for q in range(4):
+            nc.sync.dma_start(xs_s[32 * q : 32 * q + 4, :].bitcast(I32), xs_scales[0, 4 * q : 4 * q + 4, :].bitcast(I32))
+        xs_w = [load_words("xs_w%d" % g, xs_words[0][:, GATHER * g : GATHER * (g + 1), :]) for g in range(2)]
+        for a in range(2):
+            for h in range(2):
+                load_w1(a, 1, h)
+        w2_raw.append(load_words("w2_raw1", w2_words[0][:, PASS:H, :]))
+        w3_raw = []
+        for b in range(2):
+            dst = held("w3_raw%d" % b, [P, 4, N], F32)
+            nc.sync.dma_start(dst[:], w3[PASS * b : PASS * (b + 1), :].rearrange("(p j) c -> p j c", j=4))
+            w3_raw.append(dst)
+        w4_w = held("w4_w", [P, 2, 2 * N], U8)
+        nc.sync.dma_start(w4_w[:].bitcast(I32), w4_words.rearrange("a p c -> p a c").bitcast(I32))
+        for q in range(4):
+            nc.sync.dma_start(
+                w4_s[32 * q : 32 * q + 4, :, :].bitcast(I32),
+                w4_scales[:, 4 * q : 4 * q + 4, :].rearrange("a r c -> r a c").bitcast(I32),
+            )
+        swing_col = held("swing_col", [P, N_TILES], F32)
+        with nc.allow_non_contiguous_dma(reason="one value a partition"):
+            nc.sync.dma_start(swing_col[:], swing.rearrange("(n p) -> p n", p=P))
+        half_swing = held("half_swing", [P, N_TILES], F32)
+        nc.vector.tensor_scalar_mul(half_swing[:], swing_col[:], 0.5)
+
+        w2_w = {}
+
+        def order_w2(b):
+            w2_w[b] = held("w2_w%d" % b, [P, PASS], I32)
+            nc.vector.tensor_copy(w2_w[b][:].rearrange("p (t m) -> p m t", t=4), w2_raw[b][:].rearrange("p (m t) -> p m t", t=4))
+
+        order_w2(0)
+        w2_s = held("w2_s", [P, PASS], U8)
+        nc.vector.tensor_copy(w2_s[:].rearrange("p (t m) -> p m t", t=4), w2_sraw[:].rearrange("p (m t) -> p m t", t=4))
+
+        w1_w, w1_s, w1_bf = {}, {}, {}
+
+        def cast_w1(a, b):
+            grouped = held("w1_bf%d%d" % (a, b), [P, 4, P, 4], BF16)
+            for h in range(2):
+                nc.scalar.copy(
+                    grouped[:, :, 64 * h : 64 * (h + 1), :].rearrange("p t m j -> p m j t"),
+                    w1_raw[a, b, h][:].rearrange("p j (m t) -> p m j t", t=4),
+                )
+            w1_bf[a, b] = grouped
+
+        def quantize_w1(a, b):
+            w1_w[a, b] = held("w1_w%d%d" % (a, b), [P, PASS], U32)
+            w1_s[a, b] = held("w1_s%d%d" % (a, b), [P, PASS], U8)
+            nc.vector.quantize_mx(
+                out=w1_w[a, b][:].bitcast(FP8X4), scales=w1_s[a, b][:], in_=w1_bf[a, b][:].rearrange("p t m j -> p (t m j)")
+            )
+
+        v_w, v_s = {}, {}
+
+        def gather(dst, name, dtype, window, tok, width):
+            picked = held("%s_%d" % (name, tok), [P, width], dtype)
+            nc.vector.tensor_copy(picked[:], window.indirect(offsets[:, tok // 16 : (tok + width) // 16]))
+            for c in range(0, width, P):
+                dst[name, tok + c] = (picked, c)
+
+        def gather_words(a, tok, width):
+            gather(v_w, "v_w%d" % a, U32, tab_w[a][:].bitcast(U32), tok, width)
+
+        def gather_scales(tok, width):
+            gather(v_s, "v_s", U8, tab_s[:], tok, width)
+
+        cast_w1(0, 0)
+        cast_w1(1, 0)
+        gather_scales(0, 512)
+        gather_words(0, 0, 512)
+        gather_scales(512, 512)
+        quantize_w1(0, 0)
+        gather_words(0, 512, 512)
+        quantize_w1(1, 0)
+        gather_words(1, 0, 256)
+        gather_words(1, 256, 256)
+        gather_words(1, 512, 512)
+
+        feat_w, feat_s = {}, {}
+
+        def first_stage(b, tok, width):
+            g, lo = divmod(tok, GATHER)
+            soil = ring.tile([P, 4, width], F32, name="soil", tag="soil")
+            for pair in range(2):
+                bank = psum.tile([P, 2, width], F32, name="soil_bank", tag="soil_bank", bufs=2)
+                for u in range(2):
+                    t = 2 * pair + u
+                    for a in range(2):
+                        words, w0 = v_w["v_w%d" % a, tok]
+                        scales, s0 = v_s["v_s", tok]
+                        nc.tensor.matmul_mx(
+                            out=bank[:, u, :],
+                            lhsT=w1_w[a, b][:, P * t : P * (t + 1)].bitcast(FP8X4),
+                            lhsT_scale=w1_s[a, b][:, P * t : P * (t + 1)],
+                            rhs=words[:, w0 : w0 + width].bitcast(FP8X4),
+                            rhs_scale=scales[4 * a : P, s0 : s0 + width],
+                            start=(a == 0),
+                            stop=(a == 1),
+                        )
+                for u in range(2):
+                    t = 2 * pair + u
+                    nc.scalar.activation(soil[:, t, :], bank[:, u, :], ACT.Identity, bias=bias[:, b, t : t + 1])
+            feat = ring.tile([P, 2, width, 4], BF16, name="feat", tag="feat", align_bytes=64)
+            for c in range(0, width, P):
+                motor = psum.tile([P, 4, P], F32, name="motor_bank", tag="motor_bank", bufs=2)
+                for t in range(4):
+                    nc.tensor.matmul_mx(
+                        out=motor[:, t, :],
+                        lhsT=w2_w[b][:, P * t : P * (t + 1)].bitcast(FP8X4),
+                        lhsT_scale=w2_s[4 * b : P, P * t : P * (t + 1)],
+                        rhs=xs_w[g][:, lo + c : lo + c + P].bitcast(FP8X4),
+                        rhs_scale=xs_s[:, tok + c : tok + c + P],
+                        start=True,
+                        stop=True,
+                    )
+                for which, op in ((1, ALU.subtract), (0, ALU.max)):
+                    nc.vector.tensor_tensor(
+                        feat[:, which, c : c + P, :].rearrange("p (c i) t -> p c t i", i=4),
+                        soil[:, :, c : c + P].rearrange("p t (c i) -> p c t i", i=4),
+                        motor[:].rearrange("p t (c i) -> p c t i", i=4),
+                        op,
+                    )
+            return feat
+
+        def quantize_feat(b, tok, width, feat):
+            feat_w[b, tok] = held("feat_w%d_%d" % (b, tok), [P, 2, width], U32)
+            feat_s[b, tok] = held("feat_s%d_%d" % (b, tok), [P, 2, width], U8)
+            for part in ([slice(1, 2), slice(0, 1)] if tok + width == S and b == 1 else [slice(0, 2)]):
+                nc.vector.quantize_mx(
+                    out=feat_w[b, tok][:, part, :].rearrange("p w c -> p (w c)").bitcast(FP8X4),
+                    scales=feat_s[b, tok][:, part, :].rearrange("p w c -> p (w c)"),
+                    in_=feat[:, part, :, :].rearrange("p w c t -> p (w c t)"),
+                )
+
+        w3_bf = held("w3_bf", [P, 2, N, 4], BF16)
+        w3_w = held("w3_w", [P, 2 * N], U32)
+        w3_s = held("w3_s", [P, 2 * N], U8)
+
+        def cast_w3(b):
+            nc.scalar.copy(
+                w3_bf[:, b, :, :].rearrange("p (c i) j -> p c j i", i=4),
+                w3_raw[b][:].rearrange("p j (c i) -> p c j i", i=4),
+            )
+
+        def quantize_w3():
+            flat = w3_bf[:].rearrange("p b c j -> p (b c j)")
+            for lo, hi in ((0, 512), (512, 768)):
+                nc.vector.quantize_mx(out=w3_w[:, lo:hi].bitcast(FP8X4), scales=w3_s[:, lo:hi], in_=flat[:, 4 * lo : 4 * hi])
+
+        out_view = out.rearrange("(n p) s -> p n s", p=P)
+
+        def second_stage(tok, width, parts):
+            per_bank = min(512 // width, N_TILES)
+            slots = []
+            for i in range(2 * N_TILES):
+                if i % per_bank == 0:
+                    bank = psum.tile([P, per_bank, width], F32, name="y_bank", tag="y_bank", bufs=4)
+                slots.append((bank, i % per_bank))
+            y2 = slots[:N_TILES]
+            y1 = slots[N_TILES:]
+            for n in range(N_TILES):
+                bank, u = y2[n]
+                for c in range(0, width, P):
+                    for b in range(2):
+                        src, lo = parts[b]
+                        nc.tensor.matmul_mx(
+                            out=bank[:, u, c : c + P],
+                            lhsT=w4_w[:, b, 2 * P * n : 2 * P * (n + 1)].bitcast(FP4X4),
+                            lhsT_scale=w4_s[:, b, P * n : P * (n + 1)],
+                            rhs=feat_w[b, src][:, 1, lo + c : lo + c + P].bitcast(FP8X4),
+                            rhs_scale=feat_s[b, src][:, 1, lo + c : lo + c + P],
+                            start=(b == 0),
+                            stop=(b == 1),
+                        )
+            for n in range(N_TILES):
+                bank, u = y1[n]
+                for b in range(2):
+                    src, lo = parts[b]
+                    nc.tensor.matmul_mx(
+                        out=bank[:, u, :],
+                        lhsT=w3_w[:, N * b + P * n : N * b + P * (n + 1)].bitcast(FP8X4),
+                        lhsT_scale=w3_s[:, N * b + P * n : N * b + P * (n + 1)],
+                        rhs=feat_w[b, src][:, 0, lo : lo + width].bitcast(FP8X4),
+                        rhs_scale=feat_s[b, src][:, 0, lo : lo + width],
+                        start=(b == 0),
+                        stop=(b == 1),
+                    )
+
+            def runs(where):
+                found = []
+                for n in range(N_TILES):
+                    if n > 0 and where[n][1] > 0:
+                        found[-1][1] = n + 1
+                    else:
+                        found.append([n, n + 1])
+                return found
+
+            bounded = ring.tile([P, N_TILES, width], F32, name="bounded", tag="bounded", bufs=2)
+            half_sin = ring.tile([P, N_TILES, width], F32, name="half_sin", tag="half_sin", bufs=2)
+            versine = ring.tile([P, N_TILES, width], F32, name="versine", tag="versine", bufs=2)
+            result = ring.tile([P, N_TILES, width], F32, name="result", tag="result", bufs=2)
+            last = tok + width == S
+            singles = [[n, n + 1] for n in range(N_TILES)]
+            for n0, n1 in runs(y2):
+                bank, u = y2[n0]
+                nc.scalar.activation(bounded[:, n0:n1, :], bank[:, u : u + n1 - n0, :], ACT.Tanh)
+            for n in range(N_TILES):
+                nc.scalar.activation(half_sin[:, n, :], bounded[:, n, :], ACT.Sin, scale=half_swing[:, n : n + 1])
+            for n0, n1 in singles if last else runs(y1):
+                if last:
+                    nc.vector.scalar_tensor_tensor(
+                        versine[:, n0:n1, :], half_sin[:, n0:n1, :], 2.0, half_sin[:, n0:n1, :], ALU.mult, ALU.mult
+                    )
+                else:
+                    nc.scalar.activation(versine[:, n0:n1, :], half_sin[:, n0:n1, :], ACT.Square, scale=math.sqrt(2.0))
+            for n0, n1 in runs(y1):
+                bank, u = y1[n0]
+                nc.vector.scalar_tensor_tensor(
+                    result[:, n0:n1, :], versine[:, n0:n1, :], -1.0, bank[:, u : u + n1 - n0, :], ALU.add, ALU.add
+                )
+                nc.sync.dma_start(out_view[:, n0:n1, tok : tok + width], result[:, n0:n1, :])
+
+        def unit(b, tok, width):
+            quantize_feat(b, tok, width, first_stage(b, tok, width))
+
+        unit(0, 0, CHUNK)
+        cast_w1(0, 1)
+        unit(0, 256, CHUNK)
+        cast_w1(1, 1)
+        quantize_w1(0, 1)
+        unit(0, 512, CHUNK)
+        quantize_w1(1, 1)
+        order_w2(1)
+        cast_w3(0)
+        cast_w3(1)
+        unit(1, 0, CHUNK)
+        quantize_w3()
+        unit(1, 256, CHUNK)
+        second_stage(0, CHUNK, [(0, 0), (0, 0)])
+        unit(1, 512, CHUNK)
+        second_stage(256, CHUNK, [(256, 0), (256, 0)])
+        unit(0, 768, CHUNK)
+        second_stage(512, CHUNK, [(512, 0), (512, 0)])
+        unit(1, 768, 128)
+        unit(1, 896, 128)
+        second_stage(768, 128, [(768, 0), (768, 0)])
+        second_stage(896, 128, [(768, 128), (896, 0)])

@@ -40,15 +40,16 @@ def tile_list_wheel_slip_features_kernel(
         nc.sync.dma_start(offsets[:], offs)
 
         tab_s = held("tab_s", [P, T], U8)
-        nc.vector.memset(tab_s[:].bitcast(I32), 0)
+        nc.gpsimd.memset(tab_s[:].bitcast(I32), 0)
+        for q in range(4):
+            nc.gpsimd.dma_start(tab_s[32 * q : 32 * q + 8, :].bitcast(I32), tab_scales[:, 4 * q : 4 * q + 4, :].bitcast(I32))
         w2_sraw = held("w2_sraw", [P, PASS], U8)
         nc.vector.memset(w2_sraw[:].bitcast(I32), 0)
+        xs_s = held("xs_s", [P, S], U8)
+        nc.vector.memset(xs_s[:].bitcast(I32), 0)
         warm = held("warm", [P, 2], F32)
         nc.vector.memset(warm[:, 0:1], 0.0)
         nc.scalar.activation(warm[:, 1:2], warm[:, 0:1], ACT.Silu)
-
-        xs_s = held("xs_s", [P, S], U8)
-        nc.vector.memset(xs_s[:].bitcast(I32), 0)
         w4_s = held("w4_s", [P, 2, N], U8)
         nc.vector.memset(w4_s[:].rearrange("p a c -> p (a c)").bitcast(I32), 0)
 
@@ -58,42 +59,39 @@ def tile_list_wheel_slip_features_kernel(
             nc.sync.dma_start(dst[:], src.rearrange("p c i -> p (c i)").bitcast(I32))
             return dst
 
+        def load_rows(name, src):
+            dst = held(name, [P, 4, src.shape[1]], F32)
+            nc.sync.dma_start(dst[:], src.rearrange("(p j) c -> p j c", j=4))
+            return dst
+
         w1_raw = {}
 
-        def load_w1(a, b, h):
-            dst = held("w1_raw%d%d%d" % (a, b, h), [P, 4, 256], F32)
-            cols = slice(PASS * b + 256 * h, PASS * b + 256 * (h + 1))
-            nc.sync.dma_start(dst[:], w1[PASS * a : PASS * (a + 1), cols].rearrange("(p j) c -> p j c", j=4))
-            w1_raw[a, b, h] = dst
+        def load_w1(a, b):
+            w1_raw[a, b] = load_rows("w1_raw%d%d" % (a, b), w1[PASS * a : PASS * (a + 1), PASS * b : PASS * (b + 1)])
 
-        w2_raw = [load_words("w2_raw0", w2_words[0][:, 0:PASS, :])]
-        load_w1(0, 0, 0)
-        for q in range(4):
-            nc.sync.dma_start(tab_s[32 * q : 32 * q + 8, :].bitcast(I32), tab_scales[:, 4 * q : 4 * q + 4, :].bitcast(I32))
-        load_w1(0, 0, 1)
         tab_w = [load_words("tab_w0", tab_words[0])]
+        w2_all = load_words("w2_raw", w2_words[0])
+        load_w1(0, 0)
+        w2_raw = [w2_all[:, 0:PASS], w2_all[:, PASS:H]]
         for q in range(4):
             nc.sync.dma_start(
                 w2_sraw[32 * q : 32 * q + 8, :].bitcast(I32),
                 w2_scales[0, 4 * q : 4 * q + 4, :].rearrange("r (b c) -> b r c", b=2).bitcast(I32),
             )
-        load_w1(1, 0, 0)
-        load_w1(1, 0, 1)
-        tab_w.append(load_words("tab_w1", tab_words[1]))
-        bias = held("bias", [P, 2, 4], F32)
-        nc.sync.dma_start(bias[:], b1.rearrange("(b p t) -> p b t", b=2, t=4))
+        load_w1(1, 0)
         for q in range(4):
             nc.sync.dma_start(xs_s[32 * q : 32 * q + 4, :].bitcast(I32), xs_scales[0, 4 * q : 4 * q + 4, :].bitcast(I32))
-        xs_w = [load_words("xs_w%d" % g, xs_words[0][:, GATHER * g : GATHER * (g + 1), :]) for g in range(2)]
-        for a in range(2):
-            for h in range(2):
-                load_w1(a, 1, h)
-        w2_raw.append(load_words("w2_raw1", w2_words[0][:, PASS:H, :]))
-        w3_raw = []
-        for b in range(2):
-            dst = held("w3_raw%d" % b, [P, 4, N], F32)
-            nc.sync.dma_start(dst[:], w3[PASS * b : PASS * (b + 1), :].rearrange("(p j) c -> p j c", j=4))
-            w3_raw.append(dst)
+        xs_w = [load_words("xs_w0", xs_words[0][:, 0:GATHER, :])]
+        bias = held("bias", [P, 2, 4], F32)
+        nc.sync.dma_start(bias[:], b1.rearrange("(b p t) -> p b t", b=2, t=4))
+        tab_w.append(load_words("tab_w1", tab_words[1]))
+        load_w1(0, 1)
+        xs_w.append(load_words("xs_w1", xs_words[0][:, GATHER:S, :]))
+        swing_col = held("swing_col", [P, N_TILES], F32)
+        with nc.allow_non_contiguous_dma(reason="one value a partition"):
+            nc.sync.dma_start(swing_col[:], swing.rearrange("(n p) -> p n", p=P))
+        load_w1(1, 1)
+        w3_raw = [load_rows("w3_raw%d" % b, w3[PASS * b : PASS * (b + 1), :]) for b in range(2)]
         w4_w = held("w4_w", [P, 2, 2 * N], U8)
         nc.sync.dma_start(w4_w[:].bitcast(I32), w4_words.rearrange("a p c -> p a c").bitcast(I32))
         for q in range(4):
@@ -101,30 +99,26 @@ def tile_list_wheel_slip_features_kernel(
                 w4_s[32 * q : 32 * q + 4, :, :].bitcast(I32),
                 w4_scales[:, 4 * q : 4 * q + 4, :].rearrange("a r c -> r a c").bitcast(I32),
             )
-        swing_col = held("swing_col", [P, N_TILES], F32)
-        with nc.allow_non_contiguous_dma(reason="one value a partition"):
-            nc.sync.dma_start(swing_col[:], swing.rearrange("(n p) -> p n", p=P))
         half_swing = held("half_swing", [P, N_TILES], F32)
-        nc.vector.tensor_scalar_mul(half_swing[:], swing_col[:], 0.5)
+        nc.gpsimd.tensor_scalar_mul(half_swing[:], swing_col[:], 0.5)
 
         w2_w = {}
 
         def order_w2(b):
             w2_w[b] = held("w2_w%d" % b, [P, PASS], I32)
-            nc.vector.tensor_copy(w2_w[b][:].rearrange("p (t m) -> p m t", t=4), w2_raw[b][:].rearrange("p (m t) -> p m t", t=4))
+            nc.vector.tensor_copy(w2_w[b][:].rearrange("p (t m) -> p m t", t=4), w2_raw[b].rearrange("p (m t) -> p m t", t=4))
 
-        order_w2(0)
         w2_s = held("w2_s", [P, PASS], U8)
-        nc.vector.tensor_copy(w2_s[:].rearrange("p (t m) -> p m t", t=4), w2_sraw[:].rearrange("p (m t) -> p m t", t=4))
 
         w1_w, w1_s, w1_bf = {}, {}, {}
 
         def cast_w1(a, b):
-            grouped = held("w1_bf%d%d" % (a, b), [P, 4, P, 4], BF16)
+            tag = "after_unit%d" % a if b == 1 else "w1_bf%d" % a
+            grouped = keep.tile([P, 4, P, 4], BF16, name="w1_bf%d%d" % (a, b), tag=tag, align_bytes=64)
             for h in range(2):
                 nc.scalar.copy(
                     grouped[:, :, 64 * h : 64 * (h + 1), :].rearrange("p t m j -> p m j t"),
-                    w1_raw[a, b, h][:].rearrange("p j (m t) -> p m j t", t=4),
+                    w1_raw[a, b][:, :, 256 * h : 256 * (h + 1)].rearrange("p j (m t) -> p m j t", t=4),
                 )
             w1_bf[a, b] = grouped
 
@@ -151,11 +145,14 @@ def tile_list_wheel_slip_features_kernel(
 
         cast_w1(0, 0)
         cast_w1(1, 0)
-        gather_scales(0, 512)
         gather_words(0, 0, 512)
-        gather_scales(512, 512)
-        quantize_w1(0, 0)
         gather_words(0, 512, 512)
+        quantize_w1(0, 0)
+        order_w2(0)
+        order_w2(1)
+        nc.vector.tensor_copy(w2_s[:].rearrange("p (t m) -> p m t", t=4), w2_sraw[:].rearrange("p (m t) -> p m t", t=4))
+        gather_scales(0, 512)
+        gather_scales(512, 512)
         quantize_w1(1, 0)
         gather_words(1, 0, 256)
         gather_words(1, 256, 256)
@@ -165,26 +162,42 @@ def tile_list_wheel_slip_features_kernel(
 
         def first_stage(b, tok, width):
             g, lo = divmod(tok, GATHER)
-            soil = ring.tile([P, 4, width], F32, name="soil", tag="soil")
-            for pair in range(2):
-                bank = psum.tile([P, 2, width], F32, name="soil_bank", tag="soil_bank", bufs=2)
-                for u in range(2):
-                    t = 2 * pair + u
-                    for a in range(2):
-                        words, w0 = v_w["v_w%d" % a, tok]
-                        scales, s0 = v_s["v_s", tok]
-                        nc.tensor.matmul_mx(
-                            out=bank[:, u, :],
-                            lhsT=w1_w[a, b][:, P * t : P * (t + 1)].bitcast(FP8X4),
-                            lhsT_scale=w1_s[a, b][:, P * t : P * (t + 1)],
-                            rhs=words[:, w0 : w0 + width].bitcast(FP8X4),
-                            rhs_scale=scales[4 * a : P, s0 : s0 + width],
-                            start=(a == 0),
-                            stop=(a == 1),
-                        )
-                for u in range(2):
-                    t = 2 * pair + u
-                    nc.scalar.activation(soil[:, t, :], bank[:, u, :], ACT.Identity, bias=bias[:, b, t : t + 1])
+            if b == 0 and tok < 3 * CHUNK:
+                soil = keep.tile([P, 4, width], F32, name="soil", tag="after_unit%d" % (tok // CHUNK), align_bytes=64)
+            else:
+                soil = ring.tile([P, 4, width], F32, name="soil", tag="soil")
+
+            def soil_pass(dst, t, a):
+                words, w0 = v_w["v_w%d" % a, tok]
+                scales, s0 = v_s["v_s", tok]
+                nc.tensor.matmul_mx(
+                    out=dst,
+                    lhsT=w1_w[a, b][:, P * t : P * (t + 1)].bitcast(FP8X4),
+                    lhsT_scale=w1_s[a, b][:, P * t : P * (t + 1)],
+                    rhs=words[:, w0 : w0 + width].bitcast(FP8X4),
+                    rhs_scale=scales[4 * a : P, s0 : s0 + width],
+                    start=(a == 0),
+                    stop=(a == 1),
+                )
+
+            def add_bias(src, t):
+                nc.scalar.activation(soil[:, t, :], src, ACT.Identity, bias=bias[:, b, t : t + 1])
+
+            if b == 0 and tok == 0:
+                banks = [psum.tile([P, width], F32, name="first_bank", tag="y_bank", bufs=4) for t in range(4)]
+                for a in range(2):
+                    for t in range(4):
+                        soil_pass(banks[t][:], t, a)
+                for t in range(4):
+                    add_bias(banks[t][:], t)
+            else:
+                for pair in range(2):
+                    bank = psum.tile([P, 2, width], F32, name="soil_bank", tag="soil_bank", bufs=2)
+                    for u in range(2):
+                        for a in range(2):
+                            soil_pass(bank[:, u, :], 2 * pair + u, a)
+                    for u in range(2):
+                        add_bias(bank[:, u, :], 2 * pair + u)
             feat = ring.tile([P, 2, width, 4], BF16, name="feat", tag="feat", align_bytes=64)
             for c in range(0, width, P):
                 motor = psum.tile([P, 4, P], F32, name="motor_bank", tag="motor_bank", bufs=2)
@@ -217,17 +230,20 @@ def tile_list_wheel_slip_features_kernel(
                     in_=feat[:, part, :, :].rearrange("p w c t -> p (w c t)"),
                 )
 
-        w3_bf = held("w3_bf", [P, 2, N, 4], BF16)
         w3_w = held("w3_w", [P, 2 * N], U32)
         w3_s = held("w3_s", [P, 2 * N], U8)
 
-        def cast_w3(b):
-            nc.scalar.copy(
-                w3_bf[:, b, :, :].rearrange("p (c i) j -> p c j i", i=4),
-                w3_raw[b][:].rearrange("p j (c i) -> p c j i", i=4),
-            )
+        def cast_w3():
+            w3_bf = keep.tile([P, 2, N, 4], BF16, name="w3_bf", tag="after_unit2", align_bytes=64)
+            for b in range(2):
+                for cols in (slice(0, N // 2), slice(N // 2, N)):
+                    nc.scalar.copy(
+                        w3_bf[:, b, cols, :].rearrange("p (c i) j -> p c j i", i=4),
+                        w3_raw[b][:, :, cols].rearrange("p j (c i) -> p c j i", i=4),
+                    )
+            return w3_bf
 
-        def quantize_w3():
+        def quantize_w3(w3_bf):
             flat = w3_bf[:].rearrange("p b c j -> p (b c j)")
             for lo, hi in ((0, 512), (512, 768)):
                 nc.vector.quantize_mx(out=w3_w[:, lo:hi].bitcast(FP8X4), scales=w3_s[:, lo:hi], in_=flat[:, 4 * lo : 4 * hi])
@@ -315,11 +331,8 @@ def tile_list_wheel_slip_features_kernel(
         quantize_w1(0, 1)
         unit(0, 512, CHUNK)
         quantize_w1(1, 1)
-        order_w2(1)
-        cast_w3(0)
-        cast_w3(1)
         unit(1, 0, CHUNK)
-        quantize_w3()
+        quantize_w3(cast_w3())
         unit(1, 256, CHUNK)
         second_stage(0, CHUNK, [(0, 0), (0, 0)])
         unit(1, 512, CHUNK)

@@ -41,12 +41,14 @@ def tile_list_wheel_slip_features_kernel(
 
         tab_s = held("tab_s", [P, T], U8)
         nc.gpsimd.memset(tab_s[:].bitcast(I32), 0)
+        xs_s = held("xs_s", [P, S], U8)
+        nc.gpsimd.memset(xs_s[:].bitcast(I32), 0)
         for q in range(4):
             nc.gpsimd.dma_start(tab_s[32 * q : 32 * q + 8, :].bitcast(I32), tab_scales[:, 4 * q : 4 * q + 4, :].bitcast(I32))
         w2_sraw = held("w2_sraw", [P, PASS], U8)
         nc.vector.memset(w2_sraw[:].bitcast(I32), 0)
-        xs_s = held("xs_s", [P, S], U8)
-        nc.vector.memset(xs_s[:].bitcast(I32), 0)
+        for q in range(4):
+            nc.gpsimd.dma_start(xs_s[32 * q : 32 * q + 4, :].bitcast(I32), xs_scales[0, 4 * q : 4 * q + 4, :].bitcast(I32))
         warm = held("warm", [P, 2], F32)
         nc.vector.memset(warm[:, 0:1], 0.0)
         nc.scalar.activation(warm[:, 1:2], warm[:, 0:1], ACT.Silu)
@@ -67,30 +69,30 @@ def tile_list_wheel_slip_features_kernel(
         w1_raw = {}
 
         def load_w1(a, b):
-            w1_raw[a, b] = load_rows("w1_raw%d%d" % (a, b), w1[PASS * a : PASS * (a + 1), PASS * b : PASS * (b + 1)])
+            for h in range(2):
+                cols = slice(PASS * b + 256 * h, PASS * b + 256 * (h + 1))
+                w1_raw[a, b, h] = load_rows("w1_raw%d%d%d" % (a, b, h), w1[PASS * a : PASS * (a + 1), cols])
 
         tab_w = [load_words("tab_w0", tab_words[0])]
-        w2_all = load_words("w2_raw", w2_words[0])
         load_w1(0, 0)
-        w2_raw = [w2_all[:, 0:PASS], w2_all[:, PASS:H]]
         for q in range(4):
             nc.sync.dma_start(
                 w2_sraw[32 * q : 32 * q + 8, :].bitcast(I32),
                 w2_scales[0, 4 * q : 4 * q + 4, :].rearrange("r (b c) -> b r c", b=2).bitcast(I32),
             )
         load_w1(1, 0)
-        for q in range(4):
-            nc.sync.dma_start(xs_s[32 * q : 32 * q + 4, :].bitcast(I32), xs_scales[0, 4 * q : 4 * q + 4, :].bitcast(I32))
-        xs_w = [load_words("xs_w0", xs_words[0][:, 0:GATHER, :])]
         bias = held("bias", [P, 2, 4], F32)
         nc.sync.dma_start(bias[:], b1.rearrange("(b p t) -> p b t", b=2, t=4))
+        w2_raw = [load_words("w2_raw0", w2_words[0][:, 0:PASS, :])]
         tab_w.append(load_words("tab_w1", tab_words[1]))
+        xs_w = [load_words("xs_w0", xs_words[0][:, 0:GATHER, :])]
         load_w1(0, 1)
         xs_w.append(load_words("xs_w1", xs_words[0][:, GATHER:S, :]))
+        load_w1(1, 1)
+        w2_raw.append(load_words("w2_raw1", w2_words[0][:, PASS:H, :]))
         swing_col = held("swing_col", [P, N_TILES], F32)
         with nc.allow_non_contiguous_dma(reason="one value a partition"):
             nc.sync.dma_start(swing_col[:], swing.rearrange("(n p) -> p n", p=P))
-        load_w1(1, 1)
         w3_raw = [load_rows("w3_raw%d" % b, w3[PASS * b : PASS * (b + 1), :]) for b in range(2)]
         w4_w = held("w4_w", [P, 2, 2 * N], U8)
         nc.sync.dma_start(w4_w[:].bitcast(I32), w4_words.rearrange("a p c -> p a c").bitcast(I32))
@@ -106,19 +108,20 @@ def tile_list_wheel_slip_features_kernel(
 
         def order_w2(b):
             w2_w[b] = held("w2_w%d" % b, [P, PASS], I32)
-            nc.vector.tensor_copy(w2_w[b][:].rearrange("p (t m) -> p m t", t=4), w2_raw[b].rearrange("p (m t) -> p m t", t=4))
+            nc.vector.tensor_copy(w2_w[b][:].rearrange("p (t m) -> p m t", t=4), w2_raw[b][:].rearrange("p (m t) -> p m t", t=4))
 
         w2_s = held("w2_s", [P, PASS], U8)
 
         w1_w, w1_s, w1_bf = {}, {}, {}
 
         def cast_w1(a, b):
-            tag = "after_unit%d" % a if b == 1 else "w1_bf%d" % a
-            grouped = keep.tile([P, 4, P, 4], BF16, name="w1_bf%d%d" % (a, b), tag=tag, align_bytes=64)
+            grouped = held("w1_bf%d%d" % (a, b), [P, 4, P, 4], BF16)
             for h in range(2):
-                nc.scalar.copy(
+                nc.scalar.activation(
                     grouped[:, :, 64 * h : 64 * (h + 1), :].rearrange("p t m j -> p m j t"),
-                    w1_raw[a, b][:, :, 256 * h : 256 * (h + 1)].rearrange("p j (m t) -> p m j t", t=4),
+                    w1_raw[a, b, h][:].rearrange("p j (m t) -> p m j t", t=4),
+                    ACT.Copy,
+                    scale=-1.0,
                 )
             w1_bf[a, b] = grouped
 
@@ -148,172 +151,202 @@ def tile_list_wheel_slip_features_kernel(
         gather_words(0, 0, 512)
         gather_words(0, 512, 512)
         quantize_w1(0, 0)
-        order_w2(0)
-        order_w2(1)
         nc.vector.tensor_copy(w2_s[:].rearrange("p (t m) -> p m t", t=4), w2_sraw[:].rearrange("p (m t) -> p m t", t=4))
         gather_scales(0, 512)
         gather_scales(512, 512)
         quantize_w1(1, 0)
+        order_w2(0)
         gather_words(1, 0, 256)
         gather_words(1, 256, 256)
         gather_words(1, 512, 512)
 
-        feat_w, feat_s = {}, {}
+        codes, first = {}, {}
+        GAP, TOP = 0, 1
 
-        def first_stage(b, tok, width):
+        def motor_pass(dst, b, t, tok, width, start, stop):
             g, lo = divmod(tok, GATHER)
-            if b == 0 and tok < 3 * CHUNK:
-                soil = keep.tile([P, 4, width], F32, name="soil", tag="after_unit%d" % (tok // CHUNK), align_bytes=64)
-            else:
-                soil = ring.tile([P, 4, width], F32, name="soil", tag="soil")
+            nc.tensor.matmul_mx(
+                out=dst,
+                lhsT=w2_w[b][:, P * t : P * (t + 1)].bitcast(FP8X4),
+                lhsT_scale=w2_s[4 * b : P, P * t : P * (t + 1)],
+                rhs=xs_w[g][:, lo : lo + width].bitcast(FP8X4),
+                rhs_scale=xs_s[:, tok : tok + width],
+                start=start,
+                stop=stop,
+            )
 
-            def soil_pass(dst, t, a):
-                words, w0 = v_w["v_w%d" % a, tok]
-                scales, s0 = v_s["v_s", tok]
-                nc.tensor.matmul_mx(
-                    out=dst,
-                    lhsT=w1_w[a, b][:, P * t : P * (t + 1)].bitcast(FP8X4),
-                    lhsT_scale=w1_s[a, b][:, P * t : P * (t + 1)],
-                    rhs=words[:, w0 : w0 + width].bitcast(FP8X4),
-                    rhs_scale=scales[4 * a : P, s0 : s0 + width],
-                    start=(a == 0),
-                    stop=(a == 1),
-                )
+        def soil_pass(dst, b, t, a, tok, start):
+            words, w0 = v_w["v_w%d" % a, tok]
+            scales, s0 = v_s["v_s", tok]
+            nc.tensor.matmul_mx(
+                out=dst,
+                lhsT=w1_w[a, b][:, P * t : P * (t + 1)].bitcast(FP8X4),
+                lhsT_scale=w1_s[a, b][:, P * t : P * (t + 1)],
+                rhs=words[:, w0 : w0 + CHUNK].bitcast(FP8X4),
+                rhs_scale=scales[4 * a : P, s0 : s0 + CHUNK],
+                start=start,
+                stop=(a == 1),
+            )
+
+        def biased(b, tok, fused):
+            rows = held("rows%d_%d" % (b, tok), [P, 4, CHUNK], F32)
+            first[b, tok] = rows
 
             def add_bias(src, t):
-                nc.scalar.activation(soil[:, t, :], src, ACT.Identity, bias=bias[:, b, t : t + 1])
+                nc.scalar.activation(rows[:, t, :], src, ACT.Identity, bias=bias[:, b, t : t + 1], scale=-1.0)
 
             if b == 0 and tok == 0:
-                banks = [psum.tile([P, width], F32, name="first_bank", tag="y_bank", bufs=4) for t in range(4)]
+                banks = [psum.tile([P, CHUNK], F32, name="first_bank", tag=tag, bufs=3) for tag in ("y_bank", "y_bank", "y_bank", "soil_bank")]
                 for a in range(2):
                     for t in range(4):
-                        soil_pass(banks[t][:], t, a)
+                        soil_pass(banks[t][:], b, t, a, tok, a == 0)
                 for t in range(4):
                     add_bias(banks[t][:], t)
-            else:
-                for pair in range(2):
-                    bank = psum.tile([P, 2, width], F32, name="soil_bank", tag="soil_bank", bufs=2)
-                    for u in range(2):
-                        for a in range(2):
-                            soil_pass(bank[:, u, :], 2 * pair + u, a)
-                    for u in range(2):
-                        add_bias(bank[:, u, :], 2 * pair + u)
-            feat = ring.tile([P, 2, width, 4], BF16, name="feat", tag="feat", align_bytes=64)
-            for c in range(0, width, P):
-                motor = psum.tile([P, 4, P], F32, name="motor_bank", tag="motor_bank", bufs=2)
-                for t in range(4):
-                    nc.tensor.matmul_mx(
-                        out=motor[:, t, :],
-                        lhsT=w2_w[b][:, P * t : P * (t + 1)].bitcast(FP8X4),
-                        lhsT_scale=w2_s[4 * b : P, P * t : P * (t + 1)],
-                        rhs=xs_w[g][:, lo + c : lo + c + P].bitcast(FP8X4),
-                        rhs_scale=xs_s[:, tok + c : tok + c + P],
-                        start=True,
-                        stop=True,
-                    )
-                for which, op in ((1, ALU.subtract), (0, ALU.max)):
+                return
+            for pair in range(2):
+                bank = psum.tile([P, 2, CHUNK], F32, name="soil_bank", tag="soil_bank", bufs=3)
+                for u in range(2):
+                    if fused:
+                        motor_pass(bank[:, u, :], b, 2 * pair + u, tok, CHUNK, True, False)
+                    for a in range(2):
+                        soil_pass(bank[:, u, :], b, 2 * pair + u, a, tok, a == 0 and not fused)
+                for u in range(2):
+                    add_bias(bank[:, u, :], 2 * pair + u)
+
+        def motor_bank(b, tok):
+            motor = psum.tile([P, 4, P], F32, name="motor_bank", tag="motor_bank", bufs=2)
+            for t in range(4):
+                motor_pass(motor[:, t, :], b, t, tok, P, True, True)
+            return motor
+
+        def quantize_feat(feat, b, tok, kinds):
+            width = feat.shape[2]
+            name = "%d_%d_%d" % (b, tok, kinds[0])
+            words = held("feat_w" + name, [P, len(kinds), width], U32)
+            scales = held("feat_s" + name, [P, len(kinds), width], U8)
+            nc.vector.quantize_mx(
+                out=words[:].rearrange("p w c -> p (w c)").bitcast(FP8X4),
+                scales=scales[:].rearrange("p w c -> p (w c)"),
+                in_=feat.rearrange("p w c t -> p (w c t)"),
+            )
+            for w, kind in enumerate(kinds):
+                for c in range(0, width, P):
+                    codes[kind, b, tok + c] = (words[:, w, c:width], scales[:, w, c:width])
+
+        def unit(b, tok):
+            rows = first[b, tok]
+            feat = ring.tile([P, 2, CHUNK, 4], BF16, name="feat", tag="feat", align_bytes=64)
+            for c in range(0, CHUNK, P):
+                motor = motor_bank(b, tok + c)
+                for kind, op in ((GAP, ALU.subtract), (TOP, ALU.max)):
                     nc.vector.tensor_tensor(
-                        feat[:, which, c : c + P, :].rearrange("p (c i) t -> p c t i", i=4),
-                        soil[:, :, c : c + P].rearrange("p t (c i) -> p c t i", i=4),
+                        feat[:, kind, c : c + P, :].rearrange("p (c i) t -> p c t i", i=4),
+                        rows[:, :, c : c + P].rearrange("p t (c i) -> p c t i", i=4),
                         motor[:].rearrange("p t (c i) -> p c t i", i=4),
                         op,
                     )
-            return feat
+            quantize_feat(feat[:], b, tok, [GAP, TOP])
 
-        def quantize_feat(b, tok, width, feat):
-            feat_w[b, tok] = held("feat_w%d_%d" % (b, tok), [P, 2, width], U32)
-            feat_s[b, tok] = held("feat_s%d_%d" % (b, tok), [P, 2, width], U8)
-            for part in ([slice(1, 2), slice(0, 1)] if tok + width == S and b == 1 else [slice(0, 2)]):
-                nc.vector.quantize_mx(
-                    out=feat_w[b, tok][:, part, :].rearrange("p w c -> p (w c)").bitcast(FP8X4),
-                    scales=feat_s[b, tok][:, part, :].rearrange("p w c -> p (w c)"),
-                    in_=feat[:, part, :, :].rearrange("p w c t -> p (w c t)"),
+        def early_gap(b, tok, copy):
+            gap = ring.tile([P, 1, CHUNK, 4], BF16, name="gap", tag="early_gap", bufs=2, align_bytes=64)
+            copy(
+                gap[:, 0, :, :].rearrange("p (c i) t -> p c t i", i=4), first[b, tok][:].rearrange("p t (c i) -> p c t i", i=4)
+            )
+            quantize_feat(gap[:], b, tok, [GAP])
+
+        def late_top(b, chunk, lo, width):
+            top = ring.tile([P, 1, width, 4], BF16, name="top", tag="late_top", bufs=3, align_bytes=64)
+            for c in range(0, width, P):
+                nc.vector.scalar_tensor_tensor(
+                    top[:, 0, c : c + P, :],
+                    first[b, chunk][:, :, lo + c : lo + c + P].rearrange("p t c -> p c t"),
+                    0.0,
+                    motor_bank(b, chunk + lo + c)[:].rearrange("p t c -> p c t"),
+                    ALU.max,
+                    ALU.add,
                 )
+            quantize_feat(top[:], b, chunk + lo, [TOP])
 
-        w3_w = held("w3_w", [P, 2 * N], U32)
+        w3_bf = held("w3_bf", [P, 2, N, 4], BF16)
         w3_s = held("w3_s", [P, 2 * N], U8)
 
         def cast_w3():
-            w3_bf = keep.tile([P, 2, N, 4], BF16, name="w3_bf", tag="after_unit2", align_bytes=64)
             for b in range(2):
-                for cols in (slice(0, N // 2), slice(N // 2, N)):
-                    nc.scalar.copy(
-                        w3_bf[:, b, cols, :].rearrange("p (c i) j -> p c j i", i=4),
-                        w3_raw[b][:, :, cols].rearrange("p j (c i) -> p c j i", i=4),
+                for n in range(N_TILES):
+                    cols = slice(P * n, P * (n + 1))
+                    nc.gpsimd.tensor_scalar(
+                        w3_bf[:, b, cols, :], w3_raw[b][:, :, cols].rearrange("p j c -> p c j"), 1.0, 0.0, ALU.mult, ALU.add
                     )
-            return w3_bf
 
-        def quantize_w3(w3_bf):
+        def quantize_w3():
+            w3_w = held("w3_w", [P, 2 * N], U32)
             flat = w3_bf[:].rearrange("p b c j -> p (b c j)")
             for lo, hi in ((0, 512), (512, 768)):
                 nc.vector.quantize_mx(out=w3_w[:, lo:hi].bitcast(FP8X4), scales=w3_s[:, lo:hi], in_=flat[:, 4 * lo : 4 * hi])
+            return w3_w
 
         out_view = out.rearrange("(n p) s -> p n s", p=P)
 
-        def second_stage(tok, width, parts):
+        def y_slots(count, width):
             per_bank = min(512 // width, N_TILES)
             slots = []
-            for i in range(2 * N_TILES):
+            for i in range(count):
                 if i % per_bank == 0:
-                    bank = psum.tile([P, per_bank, width], F32, name="y_bank", tag="y_bank", bufs=4)
+                    bank = psum.tile([P, per_bank, width], F32, name="y_bank", tag="y_bank", bufs=3)
                 slots.append((bank, i % per_bank))
-            y2 = slots[:N_TILES]
-            y1 = slots[N_TILES:]
+            return slots
+
+        def runs(slots):
+            found = []
+            for n in range(N_TILES):
+                if n > 0 and slots[n][1] > 0:
+                    found[-1][1] = n + 1
+                else:
+                    found.append([n, n + 1])
+            return found
+
+        def versine_of(tok, width, y2):
             for n in range(N_TILES):
                 bank, u = y2[n]
                 for c in range(0, width, P):
                     for b in range(2):
-                        src, lo = parts[b]
+                        words, scales = codes[GAP, b, tok + c]
                         nc.tensor.matmul_mx(
                             out=bank[:, u, c : c + P],
                             lhsT=w4_w[:, b, 2 * P * n : 2 * P * (n + 1)].bitcast(FP4X4),
                             lhsT_scale=w4_s[:, b, P * n : P * (n + 1)],
-                            rhs=feat_w[b, src][:, 1, lo + c : lo + c + P].bitcast(FP8X4),
-                            rhs_scale=feat_s[b, src][:, 1, lo + c : lo + c + P],
+                            rhs=words[:, 0:P].bitcast(FP8X4),
+                            rhs_scale=scales[:, 0:P],
                             start=(b == 0),
                             stop=(b == 1),
                         )
-            for n in range(N_TILES):
-                bank, u = y1[n]
-                for b in range(2):
-                    src, lo = parts[b]
-                    nc.tensor.matmul_mx(
-                        out=bank[:, u, :],
-                        lhsT=w3_w[:, N * b + P * n : N * b + P * (n + 1)].bitcast(FP8X4),
-                        lhsT_scale=w3_s[:, N * b + P * n : N * b + P * (n + 1)],
-                        rhs=feat_w[b, src][:, 0, lo : lo + width].bitcast(FP8X4),
-                        rhs_scale=feat_s[b, src][:, 0, lo : lo + width],
-                        start=(b == 0),
-                        stop=(b == 1),
-                    )
-
-            def runs(where):
-                found = []
-                for n in range(N_TILES):
-                    if n > 0 and where[n][1] > 0:
-                        found[-1][1] = n + 1
-                    else:
-                        found.append([n, n + 1])
-                return found
-
             bounded = ring.tile([P, N_TILES, width], F32, name="bounded", tag="bounded", bufs=2)
             half_sin = ring.tile([P, N_TILES, width], F32, name="half_sin", tag="half_sin", bufs=2)
-            versine = ring.tile([P, N_TILES, width], F32, name="versine", tag="versine", bufs=2)
-            result = ring.tile([P, N_TILES, width], F32, name="result", tag="result", bufs=2)
-            last = tok + width == S
-            singles = [[n, n + 1] for n in range(N_TILES)]
+            versine = ring.tile([P, N_TILES, width], F32, name="versine", tag="versine", bufs=4)
             for n0, n1 in runs(y2):
                 bank, u = y2[n0]
                 nc.scalar.activation(bounded[:, n0:n1, :], bank[:, u : u + n1 - n0, :], ACT.Tanh)
             for n in range(N_TILES):
                 nc.scalar.activation(half_sin[:, n, :], bounded[:, n, :], ACT.Sin, scale=half_swing[:, n : n + 1])
-            for n0, n1 in singles if last else runs(y1):
-                if last:
-                    nc.vector.scalar_tensor_tensor(
-                        versine[:, n0:n1, :], half_sin[:, n0:n1, :], 2.0, half_sin[:, n0:n1, :], ALU.mult, ALU.mult
+            for n0, n1 in ((0, 1), (1, 3)):
+                nc.scalar.activation(versine[:, n0:n1, :], half_sin[:, n0:n1, :], ACT.Square, scale=math.sqrt(2.0))
+            return versine
+
+        def finish(tok, width, y1, versine):
+            for n in range(N_TILES):
+                bank, u = y1[n]
+                for b in range(2):
+                    words, scales = codes[TOP, b, tok]
+                    nc.tensor.matmul_mx(
+                        out=bank[:, u, :],
+                        lhsT=w3_w[:, N * b + P * n : N * b + P * (n + 1)].bitcast(FP8X4),
+                        lhsT_scale=w3_s[:, N * b + P * n : N * b + P * (n + 1)],
+                        rhs=words[:, 0:width].bitcast(FP8X4),
+                        rhs_scale=scales[:, 0:width],
+                        start=(b == 0),
+                        stop=(b == 1),
                     )
-                else:
-                    nc.scalar.activation(versine[:, n0:n1, :], half_sin[:, n0:n1, :], ACT.Square, scale=math.sqrt(2.0))
+            result = ring.tile([P, N_TILES, width], F32, name="result", tag="result", bufs=5)
             for n0, n1 in runs(y1):
                 bank, u = y1[n0]
                 nc.vector.scalar_tensor_tensor(
@@ -321,25 +354,45 @@ def tile_list_wheel_slip_features_kernel(
                 )
                 nc.sync.dma_start(out_view[:, n0:n1, tok : tok + width], result[:, n0:n1, :])
 
-        def unit(b, tok, width):
-            quantize_feat(b, tok, width, first_stage(b, tok, width))
+        def y2_stage(tok):
+            return versine_of(tok, CHUNK, y_slots(N_TILES, CHUNK))
 
-        unit(0, 0, CHUNK)
+        def y1_stage(tok, width, versine):
+            finish(tok, width, y_slots(N_TILES, width), versine)
+
+        biased(0, 0, False)
+        unit(0, 0)
+        biased(0, 256, False)
         cast_w1(0, 1)
-        unit(0, 256, CHUNK)
+        biased(0, 512, False)
         cast_w1(1, 1)
         quantize_w1(0, 1)
-        unit(0, 512, CHUNK)
+        order_w2(1)
+        unit(0, 256)
         quantize_w1(1, 1)
-        unit(1, 0, CHUNK)
-        quantize_w3(cast_w3())
-        unit(1, 256, CHUNK)
-        second_stage(0, CHUNK, [(0, 0), (0, 0)])
-        unit(1, 512, CHUNK)
-        second_stage(256, CHUNK, [(256, 0), (256, 0)])
-        unit(0, 768, CHUNK)
-        second_stage(512, CHUNK, [(512, 0), (512, 0)])
-        unit(1, 768, 128)
-        unit(1, 896, 128)
-        second_stage(768, 128, [(768, 0), (768, 0)])
-        second_stage(896, 128, [(768, 128), (896, 0)])
+        cast_w3()
+        unit(0, 512)
+        biased(0, 768, True)
+        biased(1, 0, False)
+        early_gap(0, 768, nc.scalar.copy)
+        unit(1, 0)
+        biased(1, 256, False)
+        unit(1, 256)
+        biased(1, 512, True)
+        biased(1, 768, True)
+        versine = {0: y2_stage(0)}
+        w3_w = quantize_w3()
+        early_gap(1, 512, nc.vector.tensor_copy)
+        early_gap(1, 768, nc.vector.tensor_copy)
+        versine[256] = y2_stage(256)
+        y1_stage(0, CHUNK, versine[0])
+        versine[512] = y2_stage(512)
+        late_top(1, 512, 0, CHUNK)
+        y1_stage(256, CHUNK, versine[256])
+        versine[768] = y2_stage(768)
+        late_top(0, 768, 0, CHUNK)
+        late_top(1, 768, 0, P)
+        late_top(1, 768, P, P)
+        y1_stage(512, CHUNK, versine[512])
+        for c in range(0, CHUNK, P):
+            y1_stage(768 + c, P, versine[768][:, :, c : c + P])

@@ -18,10 +18,20 @@ ACT = mybir.ActivationFunctionType
 ALU = mybir.AluOpType
 
 P = 128
-PASS = 512
-GATHER = 512
+PACK = 4
+PASS = P * PACK
+BANK = 512
+QUADS = 4
+LINE = 4
+LIST_ROWS = 16
 CHUNK = 256
+HALF_LIST = S // 2
+W1_COLS = 256
 N_TILES = N // P
+GAP, TOP = 0, 1
+
+SOIL_BANKS, MOTOR_BANKS, Y_BANKS = 3, 2, 3
+FEATURE_BUFS = 4
 
 
 def tile_list_wheel_slip_features_kernel(
@@ -30,100 +40,109 @@ def tile_list_wheel_slip_features_kernel(
     nc = tc.nc
     with ExitStack() as ctx:
         keep = ctx.enter_context(tc.tile_pool(name="keep", bufs=1))
-        ring = ctx.enter_context(tc.tile_pool(name="ring", bufs=3))
+        ring = ctx.enter_context(tc.tile_pool(name="ring", bufs=2))
         psum = ctx.enter_context(tc.psum_pool(name="psum", bufs=1))
 
         def held(name, shape, dtype):
             return keep.tile(shape, dtype, name=name, align_bytes=64)
 
-        offsets = keep.tile([P, S // 16], U16, name="offsets")
+        def mx_pass(dst, weights, weight_scales, moving, moving_scales, start, stop, weight_dtype=FP8X4):
+            nc.tensor.matmul_mx(
+                out=dst,
+                lhsT=weights.bitcast(weight_dtype),
+                lhsT_scale=weight_scales,
+                rhs=moving.bitcast(FP8X4),
+                rhs_scale=moving_scales,
+                start=start,
+                stop=stop,
+            )
+
+        offsets = keep.tile([P, S // LIST_ROWS], U16, name="offsets")
         nc.sync.dma_start(offsets[:], offs)
 
         tab_s = held("tab_s", [P, T], U8)
         nc.gpsimd.memset(tab_s[:].bitcast(I32), 0)
         xs_s = held("xs_s", [P, S], U8)
         nc.gpsimd.memset(xs_s[:].bitcast(I32), 0)
-        for q in range(4):
+        for q in range(QUADS):
             nc.gpsimd.dma_start(tab_s[32 * q : 32 * q + 8, :].bitcast(I32), tab_scales[:, 4 * q : 4 * q + 4, :].bitcast(I32))
-        w2_sraw = held("w2_sraw", [P, PASS], U8)
-        nc.vector.memset(w2_sraw[:].bitcast(I32), 0)
-        for q in range(4):
+        for q in range(QUADS):
             nc.gpsimd.dma_start(xs_s[32 * q : 32 * q + 4, :].bitcast(I32), xs_scales[0, 4 * q : 4 * q + 4, :].bitcast(I32))
-        warm = held("warm", [P, 2], F32)
-        nc.vector.memset(warm[:, 0:1], 0.0)
-        nc.scalar.activation(warm[:, 1:2], warm[:, 0:1], ACT.Silu)
+        w2_s_raw = held("w2_s_raw", [P, PASS], U8)
+        nc.vector.memset(w2_s_raw[:].bitcast(I32), 0)
+
+        silu_in = held("silu_in", [P, 1], F32)
+        nc.vector.memset(silu_in[:], 0.0)
+        zero = held("zero", [P, 1], F32)
+        nc.scalar.activation(zero[:], silu_in[:], ACT.Silu)
+
         w4_s = held("w4_s", [P, 2, N], U8)
-        nc.vector.memset(w4_s[:].rearrange("p a c -> p (a c)").bitcast(I32), 0)
+        nc.vector.memset(w4_s[:].rearrange("p b c -> p (b c)").bitcast(I32), 0)
 
         def load_words(name, src):
-            width = src.shape[1]
-            dst = held(name, [P, width], I32)
+            dst = held(name, [P, src.shape[1]], I32)
             nc.sync.dma_start(dst[:], src.rearrange("p c i -> p (c i)").bitcast(I32))
             return dst
 
         def load_rows(name, src):
-            dst = held(name, [P, 4, src.shape[1]], F32)
-            nc.sync.dma_start(dst[:], src.rearrange("(p j) c -> p j c", j=4))
+            dst = held(name, [P, PACK, src.shape[1]], F32)
+            nc.sync.dma_start(dst[:], src.rearrange("(p j) c -> p j c", j=PACK))
             return dst
 
-        w1_raw = {}
-
         def load_w1(a, b):
-            for h in range(2):
-                cols = slice(PASS * b + 256 * h, PASS * b + 256 * (h + 1))
-                w1_raw[a, b, h] = load_rows("w1_raw%d%d%d" % (a, b, h), w1[PASS * a : PASS * (a + 1), cols])
+            k_rows = w1[PASS * a : PASS * (a + 1), :]
+            starts = range(PASS * b, PASS * (b + 1), W1_COLS)
+            return [load_rows("w1_raw%d_%d" % (a, c), k_rows[:, c : c + W1_COLS]) for c in starts]
 
-        tab_w = [load_words("tab_w0", tab_words[0])]
-        load_w1(0, 0)
-        for q in range(4):
+        tab_w, w1_raw, w2_raw, xs_w = {}, {}, {}, {}
+        tab_w[0] = load_words("tab_w0", tab_words[0])
+        w1_raw[0, 0] = load_w1(0, 0)
+        for q in range(QUADS):
             nc.sync.dma_start(
-                w2_sraw[32 * q : 32 * q + 8, :].bitcast(I32),
+                w2_s_raw[32 * q : 32 * q + 8, :].bitcast(I32),
                 w2_scales[0, 4 * q : 4 * q + 4, :].rearrange("r (b c) -> b r c", b=2).bitcast(I32),
             )
-        load_w1(1, 0)
-        bias = held("bias", [P, 2, 4], F32)
-        nc.sync.dma_start(bias[:], b1.rearrange("(b p t) -> p b t", b=2, t=4))
-        w2_raw = [load_words("w2_raw0", w2_words[0][:, 0:PASS, :])]
-        tab_w.append(load_words("tab_w1", tab_words[1]))
-        xs_w = [load_words("xs_w0", xs_words[0][:, 0:GATHER, :])]
-        load_w1(0, 1)
-        xs_w.append(load_words("xs_w1", xs_words[0][:, GATHER:S, :]))
-        load_w1(1, 1)
-        w2_raw.append(load_words("w2_raw1", w2_words[0][:, PASS:H, :]))
+        w1_raw[1, 0] = load_w1(1, 0)
+        w2_raw[0] = load_words("w2_raw0", w2_words[0][:, 0:PASS, :])
+        tab_w[1] = load_words("tab_w1", tab_words[1])
+        bias = held("bias", [P, 2, PACK], F32)
+        nc.sync.dma_start(bias[:], b1.rearrange("(b p t) -> p b t", b=2, t=PACK))
+        xs_w[0] = load_words("xs_w0", xs_words[0][:, 0:HALF_LIST, :])
+        w2_raw[1] = load_words("w2_raw1", w2_words[0][:, PASS:H, :])
+        w1_raw[0, 1] = load_w1(0, 1)
+        xs_w[1] = load_words("xs_w1", xs_words[0][:, HALF_LIST:S, :])
+        w1_raw[1, 1] = load_w1(1, 1)
         swing_col = held("swing_col", [P, N_TILES], F32)
-        with nc.allow_non_contiguous_dma(reason="one value a partition"):
+        with nc.allow_non_contiguous_dma(reason="one value of swing for each partition and output tile"):
             nc.sync.dma_start(swing_col[:], swing.rearrange("(n p) -> p n", p=P))
         w3_raw = [load_rows("w3_raw%d" % b, w3[PASS * b : PASS * (b + 1), :]) for b in range(2)]
         w4_w = held("w4_w", [P, 2, 2 * N], U8)
-        nc.sync.dma_start(w4_w[:].bitcast(I32), w4_words.rearrange("a p c -> p a c").bitcast(I32))
-        for q in range(4):
+        nc.sync.dma_start(w4_w[:].bitcast(I32), w4_words.rearrange("b p c -> p b c").bitcast(I32))
+        for q in range(QUADS):
             nc.sync.dma_start(
                 w4_s[32 * q : 32 * q + 4, :, :].bitcast(I32),
-                w4_scales[:, 4 * q : 4 * q + 4, :].rearrange("a r c -> r a c").bitcast(I32),
+                w4_scales[:, 4 * q : 4 * q + 4, :].rearrange("b r c -> r b c").bitcast(I32),
             )
         half_swing = held("half_swing", [P, N_TILES], F32)
         nc.gpsimd.tensor_scalar_mul(half_swing[:], swing_col[:], 0.5)
 
-        w2_w = {}
+        w1_bf, w1_w, w1_s, w2_w = {}, {}, {}, {}
 
-        def order_w2(b):
-            w2_w[b] = held("w2_w%d" % b, [P, PASS], I32)
-            nc.vector.tensor_copy(w2_w[b][:].rearrange("p (t m) -> p m t", t=4), w2_raw[b][:].rearrange("p (m t) -> p m t", t=4))
+        def reorder_columns(name, src, dtype):
+            dst = held(name, [P, PASS], dtype)
+            nc.vector.tensor_copy(dst[:].rearrange("p (t m) -> p m t", t=PACK), src[:].rearrange("p (m t) -> p m t", t=PACK))
+            return dst
 
-        w2_s = held("w2_s", [P, PASS], U8)
-
-        w1_w, w1_s, w1_bf = {}, {}, {}
-
-        def cast_w1(a, b):
-            grouped = held("w1_bf%d%d" % (a, b), [P, 4, P, 4], BF16)
-            for h in range(2):
+        def round_w1(a, b):
+            w1_bf[a, b] = held("w1_bf%d%d" % (a, b), [P, PACK, P, PACK], BF16)
+            m_count = W1_COLS // PACK
+            for piece, raw in enumerate(w1_raw[a, b]):
                 nc.scalar.activation(
-                    grouped[:, :, 64 * h : 64 * (h + 1), :].rearrange("p t m j -> p m j t"),
-                    w1_raw[a, b, h][:].rearrange("p j (m t) -> p m j t", t=4),
+                    w1_bf[a, b][:, :, m_count * piece : m_count * (piece + 1), :].rearrange("p t m j -> p m j t"),
+                    raw[:].rearrange("p j (m t) -> p m j t", t=PACK),
                     ACT.Copy,
                     scale=-1.0,
                 )
-            w1_bf[a, b] = grouped
 
         def quantize_w1(a, b):
             w1_w[a, b] = held("w1_w%d%d" % (a, b), [P, PASS], U32)
@@ -132,145 +151,11 @@ def tile_list_wheel_slip_features_kernel(
                 out=w1_w[a, b][:].bitcast(FP8X4), scales=w1_s[a, b][:], in_=w1_bf[a, b][:].rearrange("p t m j -> p (t m j)")
             )
 
-        v_w, v_s = {}, {}
-
-        def gather(dst, name, dtype, window, tok, width):
-            picked = held("%s_%d" % (name, tok), [P, width], dtype)
-            nc.vector.tensor_copy(picked[:], window.indirect(offsets[:, tok // 16 : (tok + width) // 16]))
-            for c in range(0, width, P):
-                dst[name, tok + c] = (picked, c)
-
-        def gather_words(a, tok, width):
-            gather(v_w, "v_w%d" % a, U32, tab_w[a][:].bitcast(U32), tok, width)
-
-        def gather_scales(tok, width):
-            gather(v_s, "v_s", U8, tab_s[:], tok, width)
-
-        cast_w1(0, 0)
-        cast_w1(1, 0)
-        gather_words(0, 0, 512)
-        gather_words(0, 512, 512)
-        quantize_w1(0, 0)
-        nc.vector.tensor_copy(w2_s[:].rearrange("p (t m) -> p m t", t=4), w2_sraw[:].rearrange("p (m t) -> p m t", t=4))
-        gather_scales(0, 512)
-        gather_scales(512, 512)
-        quantize_w1(1, 0)
-        order_w2(0)
-        gather_words(1, 0, 256)
-        gather_words(1, 256, 256)
-        gather_words(1, 512, 512)
-
-        codes, first = {}, {}
-        GAP, TOP = 0, 1
-
-        def motor_pass(dst, b, t, tok, width, start, stop):
-            g, lo = divmod(tok, GATHER)
-            nc.tensor.matmul_mx(
-                out=dst,
-                lhsT=w2_w[b][:, P * t : P * (t + 1)].bitcast(FP8X4),
-                lhsT_scale=w2_s[4 * b : P, P * t : P * (t + 1)],
-                rhs=xs_w[g][:, lo : lo + width].bitcast(FP8X4),
-                rhs_scale=xs_s[:, tok : tok + width],
-                start=start,
-                stop=stop,
-            )
-
-        def soil_pass(dst, b, t, a, tok, start):
-            words, w0 = v_w["v_w%d" % a, tok]
-            scales, s0 = v_s["v_s", tok]
-            nc.tensor.matmul_mx(
-                out=dst,
-                lhsT=w1_w[a, b][:, P * t : P * (t + 1)].bitcast(FP8X4),
-                lhsT_scale=w1_s[a, b][:, P * t : P * (t + 1)],
-                rhs=words[:, w0 : w0 + CHUNK].bitcast(FP8X4),
-                rhs_scale=scales[4 * a : P, s0 : s0 + CHUNK],
-                start=start,
-                stop=(a == 1),
-            )
-
-        def biased(b, tok, fused):
-            rows = held("rows%d_%d" % (b, tok), [P, 4, CHUNK], F32)
-            first[b, tok] = rows
-
-            def add_bias(src, t):
-                nc.scalar.activation(rows[:, t, :], src, ACT.Identity, bias=bias[:, b, t : t + 1], scale=-1.0)
-
-            if b == 0 and tok == 0:
-                banks = [psum.tile([P, CHUNK], F32, name="first_bank", tag=tag, bufs=3) for tag in ("y_bank", "y_bank", "y_bank", "soil_bank")]
-                for a in range(2):
-                    for t in range(4):
-                        soil_pass(banks[t][:], b, t, a, tok, a == 0)
-                for t in range(4):
-                    add_bias(banks[t][:], t)
-                return
-            for pair in range(2):
-                bank = psum.tile([P, 2, CHUNK], F32, name="soil_bank", tag="soil_bank", bufs=3)
-                for u in range(2):
-                    if fused:
-                        motor_pass(bank[:, u, :], b, 2 * pair + u, tok, CHUNK, True, False)
-                    for a in range(2):
-                        soil_pass(bank[:, u, :], b, 2 * pair + u, a, tok, a == 0 and not fused)
-                for u in range(2):
-                    add_bias(bank[:, u, :], 2 * pair + u)
-
-        def motor_bank(b, tok):
-            motor = psum.tile([P, 4, P], F32, name="motor_bank", tag="motor_bank", bufs=2)
-            for t in range(4):
-                motor_pass(motor[:, t, :], b, t, tok, P, True, True)
-            return motor
-
-        def quantize_feat(feat, b, tok, kinds):
-            width = feat.shape[2]
-            name = "%d_%d_%d" % (b, tok, kinds[0])
-            words = held("feat_w" + name, [P, len(kinds), width], U32)
-            scales = held("feat_s" + name, [P, len(kinds), width], U8)
-            nc.vector.quantize_mx(
-                out=words[:].rearrange("p w c -> p (w c)").bitcast(FP8X4),
-                scales=scales[:].rearrange("p w c -> p (w c)"),
-                in_=feat.rearrange("p w c t -> p (w c t)"),
-            )
-            for w, kind in enumerate(kinds):
-                for c in range(0, width, P):
-                    codes[kind, b, tok + c] = (words[:, w, c:width], scales[:, w, c:width])
-
-        def unit(b, tok):
-            rows = first[b, tok]
-            feat = ring.tile([P, 2, CHUNK, 4], BF16, name="feat", tag="feat", align_bytes=64)
-            for c in range(0, CHUNK, P):
-                motor = motor_bank(b, tok + c)
-                for kind, op in ((GAP, ALU.subtract), (TOP, ALU.max)):
-                    nc.vector.tensor_tensor(
-                        feat[:, kind, c : c + P, :].rearrange("p (c i) t -> p c t i", i=4),
-                        rows[:, :, c : c + P].rearrange("p t (c i) -> p c t i", i=4),
-                        motor[:].rearrange("p t (c i) -> p c t i", i=4),
-                        op,
-                    )
-            quantize_feat(feat[:], b, tok, [GAP, TOP])
-
-        def early_gap(b, tok, copy):
-            gap = ring.tile([P, 1, CHUNK, 4], BF16, name="gap", tag="early_gap", bufs=2, align_bytes=64)
-            copy(
-                gap[:, 0, :, :].rearrange("p (c i) t -> p c t i", i=4), first[b, tok][:].rearrange("p t (c i) -> p c t i", i=4)
-            )
-            quantize_feat(gap[:], b, tok, [GAP])
-
-        def late_top(b, chunk, lo, width):
-            top = ring.tile([P, 1, width, 4], BF16, name="top", tag="late_top", bufs=3, align_bytes=64)
-            for c in range(0, width, P):
-                nc.vector.scalar_tensor_tensor(
-                    top[:, 0, c : c + P, :],
-                    first[b, chunk][:, :, lo + c : lo + c + P].rearrange("p t c -> p c t"),
-                    0.0,
-                    motor_bank(b, chunk + lo + c)[:].rearrange("p t c -> p c t"),
-                    ALU.max,
-                    ALU.add,
-                )
-            quantize_feat(top[:], b, chunk + lo, [TOP])
-
-        w3_bf = held("w3_bf", [P, 2, N, 4], BF16)
+        w3_bf = held("w3_bf", [P, 2, N, PACK], BF16)
+        w3_w = held("w3_w", [P, 2 * N], U32)
         w3_s = held("w3_s", [P, 2 * N], U8)
 
-        def cast_w3():
+        def round_w3():
             for b in range(2):
                 for n in range(N_TILES):
                     cols = slice(P * n, P * (n + 1))
@@ -279,120 +164,233 @@ def tile_list_wheel_slip_features_kernel(
                     )
 
         def quantize_w3():
-            w3_w = held("w3_w", [P, 2 * N], U32)
             flat = w3_bf[:].rearrange("p b c j -> p (b c j)")
-            for lo, hi in ((0, 512), (512, 768)):
-                nc.vector.quantize_mx(out=w3_w[:, lo:hi].bitcast(FP8X4), scales=w3_s[:, lo:hi], in_=flat[:, 4 * lo : 4 * hi])
-            return w3_w
+            for lo, hi in ((0, PASS), (PASS, 2 * N)):
+                nc.vector.quantize_mx(out=w3_w[:, lo:hi].bitcast(FP8X4), scales=w3_s[:, lo:hi], in_=flat[:, PACK * lo : PACK * hi])
+
+        picked = {}
+
+        def gather(name, dtype, window, entry, count):
+            dst = held("%s_%d" % (name, entry), [P, count], dtype)
+            nc.vector.tensor_copy(dst[:], window.indirect(offsets[:, entry // LIST_ROWS : (entry + count) // LIST_ROWS]))
+            for c in range(0, count, CHUNK):
+                picked[name, entry + c] = dst[:, c : c + CHUNK]
+
+        def gather_words(a, entry, count):
+            gather("v_w%d" % a, U32, tab_w[a][:].bitcast(U32), entry, count)
+
+        round_w1(0, 0)
+        round_w1(1, 0)
+        for entry in (0, HALF_LIST):
+            gather_words(0, entry, HALF_LIST)
+        quantize_w1(0, 0)
+        w2_s = reorder_columns("w2_s", w2_s_raw, U8)
+        for entry in (0, HALF_LIST):
+            gather("v_s", U8, tab_s[:], entry, HALF_LIST)
+        quantize_w1(1, 0)
+        w2_w[0] = reorder_columns("w2_w0", w2_raw[0], I32)
+        gather_words(1, 0, CHUNK)
+        gather_words(1, CHUNK, CHUNK)
+        gather_words(1, HALF_LIST, HALF_LIST)
+
+        biased = {}
+        features = {}
+
+        def motor_pass(dst, b, t, entry, count, stop):
+            half, lo = divmod(entry, HALF_LIST)
+            cols = slice(P * t, P * (t + 1))
+            mx_pass(dst, w2_w[b][:, cols], w2_s[4 * b : P, cols], xs_w[half][:, lo : lo + count], xs_s[:, entry : entry + count], True, stop)
+
+        def soil_pass(dst, b, t, a, chunk, start):
+            cols = slice(P * t, P * (t + 1))
+            words, scales = picked["v_w%d" % a, chunk], picked["v_s", chunk][4 * a : P, :]
+            mx_pass(dst, w1_w[a, b][:, cols], w1_s[a, b][:, cols], words, scales, start, a == 1)
+
+        def add_bias(b, chunk, t, sums):
+            nc.scalar.activation(biased[b, chunk][:, t, :], sums, ACT.Identity, bias=bias[:, b, t : t + 1], scale=-1.0)
+
+        def first_soil_rows():
+            biased[0, 0] = held("biased0_0", [P, PACK, CHUNK], F32)
+            banks = [psum.tile([P, CHUNK], F32, name="first_bank", tag="y_bank", bufs=Y_BANKS) for t in range(Y_BANKS)]
+            banks.append(psum.tile([P, CHUNK], F32, name="first_bank", tag="soil_bank", bufs=SOIL_BANKS))
+            for a in range(2):
+                for t in range(PACK):
+                    soil_pass(banks[t][:], 0, t, a, 0, a == 0)
+            for t in range(PACK):
+                add_bias(0, 0, t, banks[t][:])
+
+        def biased_rows(b, chunk, kind):
+            biased[b, chunk] = held("biased%d_%d" % (b, chunk), [P, PACK, CHUNK], F32)
+            with_motor = kind == "gap"
+            for t0 in range(0, PACK, BANK // CHUNK):
+                bank = psum.tile([P, BANK // CHUNK, CHUNK], F32, name="soil_bank", tag="soil_bank", bufs=SOIL_BANKS)
+                for u in range(BANK // CHUNK):
+                    if with_motor:
+                        motor_pass(bank[:, u, :], b, t0 + u, chunk, CHUNK, False)
+                    for a in range(2):
+                        soil_pass(bank[:, u, :], b, t0 + u, a, chunk, a == 0 and not with_motor)
+                for u in range(BANK // CHUNK):
+                    add_bias(b, chunk, t0 + u, bank[:, u, :])
+
+        def motor_bank(b, entry):
+            bank = psum.tile([P, PACK, P], F32, name="motor_bank", tag="motor_bank", bufs=MOTOR_BANKS)
+            for t in range(PACK):
+                motor_pass(bank[:, t, :], b, t, entry, P, True)
+            return bank
+
+        def feature_tile(kinds, count):
+            return ring.tile([P, len(kinds), count, PACK], BF16, name="feature", tag="feature", bufs=FEATURE_BUFS, align_bytes=64)
+
+        def biased_part(b, entry, count):
+            chunk, lo = entry - entry % CHUNK, entry % CHUNK
+            return biased[b, chunk][:, :, lo : lo + count]
+
+        def by_lines(planar):
+            return planar.rearrange("p t (c i) -> p c t i", i=LINE)
+
+        def by_lines_interleaved(words):
+            return words.rearrange("p (c i) t -> p c t i", i=LINE)
+
+        def quantize_features(values, b, entry, kinds):
+            count = values.shape[2]
+            name = "%d_%d_%d" % (kinds[0], b, entry)
+            words = held("feature_w" + name, [P, len(kinds), count], U32)
+            scales = held("feature_s" + name, [P, len(kinds), count], U8)
+            nc.vector.quantize_mx(
+                out=words[:].rearrange("p w c -> p (w c)").bitcast(FP8X4),
+                scales=scales[:].rearrange("p w c -> p (w c)"),
+                in_=values[:].rearrange("p w c t -> p (w c t)"),
+            )
+            for w, kind in enumerate(kinds):
+                for c in range(0, count, P):
+                    features[kind, b, entry + c] = (words[:, w, c:count], scales[:, w, c:count])
+
+        def features_from_soil(b, entry, count, kinds):
+            values = feature_tile(kinds, count)
+            for c in range(0, count, P):
+                motor = motor_bank(b, entry + c)
+                for w, kind in enumerate(kinds):
+                    nc.vector.tensor_tensor(
+                        by_lines_interleaved(values[:, w, c : c + P, :]),
+                        by_lines(biased_part(b, entry + c, P)),
+                        by_lines(motor[:]),
+                        ALU.subtract if kind == GAP else ALU.max,
+                    )
+            quantize_features(values, b, entry, kinds)
+
+        def gap_from_gap_rows(b, chunk):
+            values = feature_tile([GAP], CHUNK)
+            nc.scalar.copy(by_lines_interleaved(values[:, 0, :, :]), by_lines(biased[b, chunk][:]))
+            quantize_features(values, b, chunk, [GAP])
+
+        def top_from_gap_rows(b, entry, count):
+            values = feature_tile([TOP], count)
+            for c in range(0, count, P):
+                nc.vector.scalar_tensor_tensor(
+                    values[:, 0, c : c + P, :],
+                    biased_part(b, entry + c, P).rearrange("p t c -> p c t"),
+                    0.0,
+                    motor_bank(b, entry + c)[:].rearrange("p t c -> p c t"),
+                    ALU.max,
+                    ALU.add,
+                )
+            quantize_features(values, b, entry, [TOP])
 
         out_view = out.rearrange("(n p) s -> p n s", p=P)
+        versine = {}
 
-        def y_slots(count, width):
-            per_bank = min(512 // width, N_TILES)
-            slots = []
-            for i in range(count):
-                if i % per_bank == 0:
-                    bank = psum.tile([P, per_bank, width], F32, name="y_bank", tag="y_bank", bufs=3)
-                slots.append((bank, i % per_bank))
-            return slots
+        def y_banks(count):
+            per_bank = min(BANK // count, N_TILES)
+            groups = []
+            for n0 in range(0, N_TILES, per_bank):
+                bank = psum.tile([P, per_bank, count], F32, name="y_bank", tag="y_bank", bufs=Y_BANKS)
+                groups.append((bank, n0, min(per_bank, N_TILES - n0)))
+            return groups
 
-        def runs(slots):
-            found = []
+        def versine_rows(chunk):
+            groups = y_banks(CHUNK)
+            for bank, n0, tiles in groups:
+                for n in range(n0, n0 + tiles):
+                    for c in range(0, CHUNK, P):
+                        for b in range(2):
+                            words, scales = features[GAP, b, chunk + c]
+                            mx_pass(
+                                bank[:, n - n0, c : c + P],
+                                w4_w[:, b, 2 * P * n : 2 * P * (n + 1)],
+                                w4_s[:, b, P * n : P * (n + 1)],
+                                words[:, 0:P],
+                                scales[:, 0:P],
+                                b == 0,
+                                b == 1,
+                                FP4X4,
+                            )
+            bounded = ring.tile([P, N_TILES, CHUNK], F32, name="bounded", tag="bounded")
+            half_sin = ring.tile([P, N_TILES, CHUNK], F32, name="half_sin", tag="half_sin")
+            versine[chunk] = held("versine%d" % chunk, [P, N_TILES, CHUNK], F32)
+            for bank, n0, tiles in groups:
+                nc.scalar.activation(bounded[:, n0 : n0 + tiles, :], bank[:, 0:tiles, :], ACT.Tanh)
             for n in range(N_TILES):
-                if n > 0 and slots[n][1] > 0:
-                    found[-1][1] = n + 1
-                else:
-                    found.append([n, n + 1])
-            return found
+                nc.scalar.activation(half_sin[:, n, :], bounded[:, n, :], ACT.Sin, bias=zero[:], scale=half_swing[:, n : n + 1])
+            for tiles in (slice(0, 1), slice(1, N_TILES)):
+                nc.scalar.activation(versine[chunk][:, tiles, :], half_sin[:, tiles, :], ACT.Square, scale=math.sqrt(2.0))
 
-        def versine_of(tok, width, y2):
-            for n in range(N_TILES):
-                bank, u = y2[n]
-                for c in range(0, width, P):
+        def finish(entry, count):
+            chunk, lo = entry - entry % CHUNK, entry % CHUNK
+            groups = y_banks(count)
+            for bank, n0, tiles in groups:
+                for n in range(n0, n0 + tiles):
                     for b in range(2):
-                        words, scales = codes[GAP, b, tok + c]
-                        nc.tensor.matmul_mx(
-                            out=bank[:, u, c : c + P],
-                            lhsT=w4_w[:, b, 2 * P * n : 2 * P * (n + 1)].bitcast(FP4X4),
-                            lhsT_scale=w4_s[:, b, P * n : P * (n + 1)],
-                            rhs=words[:, 0:P].bitcast(FP8X4),
-                            rhs_scale=scales[:, 0:P],
-                            start=(b == 0),
-                            stop=(b == 1),
-                        )
-            bounded = ring.tile([P, N_TILES, width], F32, name="bounded", tag="bounded", bufs=2)
-            half_sin = ring.tile([P, N_TILES, width], F32, name="half_sin", tag="half_sin", bufs=2)
-            versine = ring.tile([P, N_TILES, width], F32, name="versine", tag="versine", bufs=4)
-            for n0, n1 in runs(y2):
-                bank, u = y2[n0]
-                nc.scalar.activation(bounded[:, n0:n1, :], bank[:, u : u + n1 - n0, :], ACT.Tanh)
-            for n in range(N_TILES):
-                nc.scalar.activation(half_sin[:, n, :], bounded[:, n, :], ACT.Sin, scale=half_swing[:, n : n + 1])
-            for n0, n1 in ((0, 1), (1, 3)):
-                nc.scalar.activation(versine[:, n0:n1, :], half_sin[:, n0:n1, :], ACT.Square, scale=math.sqrt(2.0))
-            return versine
-
-        def finish(tok, width, y1, versine):
-            for n in range(N_TILES):
-                bank, u = y1[n]
-                for b in range(2):
-                    words, scales = codes[TOP, b, tok]
-                    nc.tensor.matmul_mx(
-                        out=bank[:, u, :],
-                        lhsT=w3_w[:, N * b + P * n : N * b + P * (n + 1)].bitcast(FP8X4),
-                        lhsT_scale=w3_s[:, N * b + P * n : N * b + P * (n + 1)],
-                        rhs=words[:, 0:width].bitcast(FP8X4),
-                        rhs_scale=scales[:, 0:width],
-                        start=(b == 0),
-                        stop=(b == 1),
-                    )
-            result = ring.tile([P, N_TILES, width], F32, name="result", tag="result", bufs=5)
-            for n0, n1 in runs(y1):
-                bank, u = y1[n0]
+                        words, scales = features[TOP, b, entry]
+                        cols = slice(N * b + P * n, N * b + P * (n + 1))
+                        mx_pass(bank[:, n - n0, :], w3_w[:, cols], w3_s[:, cols], words[:, 0:count], scales[:, 0:count], b == 0, b == 1)
+            result = held("result%d" % entry, [P, N_TILES, count], F32)
+            for bank, n0, tiles in groups:
+                rows = slice(n0, n0 + tiles)
                 nc.vector.scalar_tensor_tensor(
-                    result[:, n0:n1, :], versine[:, n0:n1, :], -1.0, bank[:, u : u + n1 - n0, :], ALU.add, ALU.add
+                    result[:, rows, :], versine[chunk][:, rows, lo : lo + count], -1.0, bank[:, 0:tiles, :], ALU.add, ALU.add
                 )
-                nc.sync.dma_start(out_view[:, n0:n1, tok : tok + width], result[:, n0:n1, :])
+                nc.sync.dma_start(out_view[:, rows, entry : entry + count], result[:, rows, :])
 
-        def y2_stage(tok):
-            return versine_of(tok, CHUNK, y_slots(N_TILES, CHUNK))
+        c0, c1, c2, c3 = range(0, S, CHUNK)
+        both = [GAP, TOP]
 
-        def y1_stage(tok, width, versine):
-            finish(tok, width, y_slots(N_TILES, width), versine)
-
-        biased(0, 0, False)
-        unit(0, 0)
-        biased(0, 256, False)
-        cast_w1(0, 1)
-        biased(0, 512, False)
-        cast_w1(1, 1)
+        first_soil_rows()
+        w2_w[1] = reorder_columns("w2_w1", w2_raw[1], I32)
+        features_from_soil(0, c0, CHUNK, both)
+        biased_rows(0, c1, "soil")
+        round_w1(0, 1)
+        biased_rows(0, c2, "soil")
+        round_w1(1, 1)
         quantize_w1(0, 1)
-        order_w2(1)
-        unit(0, 256)
+        features_from_soil(0, c1, CHUNK, both)
         quantize_w1(1, 1)
-        cast_w3()
-        unit(0, 512)
-        biased(0, 768, True)
-        biased(1, 0, False)
-        early_gap(0, 768, nc.scalar.copy)
-        unit(1, 0)
-        biased(1, 256, False)
-        unit(1, 256)
-        biased(1, 512, True)
-        biased(1, 768, True)
-        versine = {0: y2_stage(0)}
-        w3_w = quantize_w3()
-        early_gap(1, 512, nc.vector.tensor_copy)
-        early_gap(1, 768, nc.vector.tensor_copy)
-        versine[256] = y2_stage(256)
-        y1_stage(0, CHUNK, versine[0])
-        versine[512] = y2_stage(512)
-        late_top(1, 512, 0, CHUNK)
-        y1_stage(256, CHUNK, versine[256])
-        versine[768] = y2_stage(768)
-        late_top(0, 768, 0, CHUNK)
-        late_top(1, 768, 0, P)
-        late_top(1, 768, P, P)
-        y1_stage(512, CHUNK, versine[512])
-        for c in range(0, CHUNK, P):
-            y1_stage(768 + c, P, versine[768][:, :, c : c + P])
+        round_w3()
+        features_from_soil(0, c2, CHUNK, both)
+
+        biased_rows(0, c3, "gap")
+        biased_rows(1, c0, "soil")
+        gap_from_gap_rows(0, c3)
+        top_from_gap_rows(0, c3, P)
+
+        features_from_soil(1, c0, CHUNK, both)
+        biased_rows(1, c1, "soil")
+        features_from_soil(1, c1, CHUNK, both)
+        biased_rows(1, c2, "gap")
+        gap_from_gap_rows(1, c2)
+        biased_rows(1, c3, "soil")
+        versine_rows(c0)
+        quantize_w3()
+        features_from_soil(1, c3, CHUNK, [GAP])
+
+        versine_rows(c1)
+        finish(c0, CHUNK)
+        versine_rows(c2)
+        top_from_gap_rows(1, c2, CHUNK)
+        finish(c1, CHUNK)
+        versine_rows(c3)
+        top_from_gap_rows(0, c3 + P, P)
+        for entry in (c3, c3 + P):
+            features_from_soil(1, entry, P, [TOP])
+        finish(c2, CHUNK)
+        for entry in (c3, c3 + P):
+            finish(entry, P)

import math
from contextlib import ExitStack

import concourse.mybir as mybir

K, K2, H, N, T, S = 1024, 512, 1024, 384, 2048, 1024
FLOPS = 2 * S * (K * H + K2 * H + 2 * H * N)

F32 = mybir.dt.float32
BF16 = mybir.dt.bfloat16
I32 = mybir.dt.int32
U32 = mybir.dt.uint32
U16 = mybir.dt.uint16
U8 = mybir.dt.uint8
FP8X4 = mybir.dt.float8_e4m3fn_x4
FP4X4 = mybir.dt.float4_e2m1fn_x4
ACT = mybir.ActivationFunctionType
ALU = mybir.AluOpType

P = 128
PACK = 4
PASS = P * PACK
BANK = 512
QUADS = 4
LINE = 4
LIST_ROWS = 16
CHUNK = 256
HALF_LIST = S // 2
W1_COLS = 256
N_TILES = N // P
GAP, TOP = 0, 1

SOIL_BANKS, MOTOR_BANKS, Y_BANKS = 3, 2, 3
FEATURE_BUFS = 4


def tile_list_wheel_slip_features_kernel(
    tc, tab_words, tab_scales, offs, xs_words, xs_scales, w1, b1, w2_words, w2_scales, w3, w4_words, w4_scales, swing, out
):
    nc = tc.nc
    with ExitStack() as ctx:
        keep = ctx.enter_context(tc.tile_pool(name="keep", bufs=1))
        ring = ctx.enter_context(tc.tile_pool(name="ring", bufs=2))
        psum = ctx.enter_context(tc.psum_pool(name="psum", bufs=1))

        def held(name, shape, dtype):
            return keep.tile(shape, dtype, name=name, align_bytes=64)

        def mx_pass(dst, weights, weight_scales, moving, moving_scales, start, stop, weight_dtype=FP8X4):
            nc.tensor.matmul_mx(
                out=dst,
                lhsT=weights.bitcast(weight_dtype),
                lhsT_scale=weight_scales,
                rhs=moving.bitcast(FP8X4),
                rhs_scale=moving_scales,
                start=start,
                stop=stop,
            )

        offsets = keep.tile([P, S // LIST_ROWS], U16, name="offsets")
        nc.sync.dma_start(offsets[:], offs)

        tab_s = held("tab_s", [P, T], U8)
        nc.gpsimd.memset(tab_s[:].bitcast(I32), 0)
        xs_s = held("xs_s", [P, S], U8)
        nc.gpsimd.memset(xs_s[:].bitcast(I32), 0)
        for q in range(QUADS):
            nc.gpsimd.dma_start(tab_s[32 * q : 32 * q + 8, :].bitcast(I32), tab_scales[:, 4 * q : 4 * q + 4, :].bitcast(I32))
        for q in range(QUADS):
            nc.gpsimd.dma_start(xs_s[32 * q : 32 * q + 4, :].bitcast(I32), xs_scales[0, 4 * q : 4 * q + 4, :].bitcast(I32))
        w2_s_raw = held("w2_s_raw", [P, PASS], U8)
        nc.vector.memset(w2_s_raw[:].bitcast(I32), 0)

        silu_in = held("silu_in", [P, 1], F32)
        nc.vector.memset(silu_in[:], 0.0)
        zero = held("zero", [P, 1], F32)
        nc.scalar.activation(zero[:], silu_in[:], ACT.Silu)

        w4_s = held("w4_s", [P, 2, N], U8)
        nc.vector.memset(w4_s[:].rearrange("p b c -> p (b c)").bitcast(I32), 0)

        def load_words(name, src):
            dst = held(name, [P, src.shape[1]], I32)
            nc.sync.dma_start(dst[:], src.rearrange("p c i -> p (c i)").bitcast(I32))
            return dst

        def load_rows(name, src):
            dst = held(name, [P, PACK, src.shape[1]], F32)
            nc.sync.dma_start(dst[:], src.rearrange("(p j) c -> p j c", j=PACK))
            return dst

        def load_w1(a, b):
            k_rows = w1[PASS * a : PASS * (a + 1), :]
            starts = range(PASS * b, PASS * (b + 1), W1_COLS)
            return [load_rows("w1_raw%d_%d" % (a, c), k_rows[:, c : c + W1_COLS]) for c in starts]

        tab_w, w1_raw, w2_raw, xs_w = {}, {}, {}, {}
        tab_w[0] = load_words("tab_w0", tab_words[0])
        w1_raw[0, 0] = load_w1(0, 0)
        for q in range(QUADS):
            nc.sync.dma_start(
                w2_s_raw[32 * q : 32 * q + 8, :].bitcast(I32),
                w2_scales[0, 4 * q : 4 * q + 4, :].rearrange("r (b c) -> b r c", b=2).bitcast(I32),
            )
        w1_raw[1, 0] = load_w1(1, 0)
        w2_raw[0] = load_words("w2_raw0", w2_words[0][:, 0:PASS, :])
        tab_w[1] = load_words("tab_w1", tab_words[1])
        bias = held("bias", [P, 2, PACK], F32)
        nc.sync.dma_start(bias[:], b1.rearrange("(b p t) -> p b t", b=2, t=PACK))
        xs_w[0] = load_words("xs_w0", xs_words[0][:, 0:HALF_LIST, :])
        w2_raw[1] = load_words("w2_raw1", w2_words[0][:, PASS:H, :])
        w1_raw[0, 1] = load_w1(0, 1)
        xs_w[1] = load_words("xs_w1", xs_words[0][:, HALF_LIST:S, :])
        w1_raw[1, 1] = load_w1(1, 1)
        swing_col = held("swing_col", [P, N_TILES], F32)
        with nc.allow_non_contiguous_dma(reason="one value of swing for each partition and output tile"):
            nc.sync.dma_start(swing_col[:], swing.rearrange("(n p) -> p n", p=P))
        w3_raw = [load_rows("w3_raw%d" % b, w3[PASS * b : PASS * (b + 1), :]) for b in range(2)]
        w4_w = held("w4_w", [P, 2, 2 * N], U8)
        nc.sync.dma_start(w4_w[:].bitcast(I32), w4_words.rearrange("b p c -> p b c").bitcast(I32))
        for q in range(QUADS):
            nc.sync.dma_start(
                w4_s[32 * q : 32 * q + 4, :, :].bitcast(I32),
                w4_scales[:, 4 * q : 4 * q + 4, :].rearrange("b r c -> r b c").bitcast(I32),
            )
        half_swing = held("half_swing", [P, N_TILES], F32)
        nc.gpsimd.tensor_scalar_mul(half_swing[:], swing_col[:], 0.5)

        w1_bf, w1_w, w1_s, w2_w = {}, {}, {}, {}

        def reorder_columns(name, src, dtype):
            dst = held(name, [P, PASS], dtype)
            nc.vector.tensor_copy(dst[:].rearrange("p (t m) -> p m t", t=PACK), src[:].rearrange("p (m t) -> p m t", t=PACK))
            return dst

        def round_w1(a, b):
            w1_bf[a, b] = held("w1_bf%d%d" % (a, b), [P, PACK, P, PACK], BF16)
            m_count = W1_COLS // PACK
            for piece, raw in enumerate(w1_raw[a, b]):
                nc.scalar.activation(
                    w1_bf[a, b][:, :, m_count * piece : m_count * (piece + 1), :].rearrange("p t m j -> p m j t"),
                    raw[:].rearrange("p j (m t) -> p m j t", t=PACK),
                    ACT.Copy,
                    scale=-1.0,
                )

        def quantize_w1(a, b):
            w1_w[a, b] = held("w1_w%d%d" % (a, b), [P, PASS], U32)
            w1_s[a, b] = held("w1_s%d%d" % (a, b), [P, PASS], U8)
            nc.vector.quantize_mx(
                out=w1_w[a, b][:].bitcast(FP8X4), scales=w1_s[a, b][:], in_=w1_bf[a, b][:].rearrange("p t m j -> p (t m j)")
            )

        w3_bf = held("w3_bf", [P, 2, N, PACK], BF16)
        w3_w = held("w3_w", [P, 2 * N], U32)
        w3_s = held("w3_s", [P, 2 * N], U8)

        def round_w3():
            for b in range(2):
                for n in range(N_TILES):
                    cols = slice(P * n, P * (n + 1))
                    nc.gpsimd.tensor_scalar(
                        w3_bf[:, b, cols, :], w3_raw[b][:, :, cols].rearrange("p j c -> p c j"), 1.0, 0.0, ALU.mult, ALU.add
                    )

        def quantize_w3():
            flat = w3_bf[:].rearrange("p b c j -> p (b c j)")
            for lo, hi in ((0, PASS), (PASS, 2 * N)):
                nc.vector.quantize_mx(out=w3_w[:, lo:hi].bitcast(FP8X4), scales=w3_s[:, lo:hi], in_=flat[:, PACK * lo : PACK * hi])

        picked = {}

        def gather(name, dtype, window, entry, count):
            dst = held("%s_%d" % (name, entry), [P, count], dtype)
            nc.vector.tensor_copy(dst[:], window.indirect(offsets[:, entry // LIST_ROWS : (entry + count) // LIST_ROWS]))
            for c in range(0, count, CHUNK):
                picked[name, entry + c] = dst[:, c : c + CHUNK]

        def gather_words(a, entry, count):
            gather("v_w%d" % a, U32, tab_w[a][:].bitcast(U32), entry, count)

        round_w1(0, 0)
        round_w1(1, 0)
        for entry in (0, HALF_LIST):
            gather_words(0, entry, HALF_LIST)
        quantize_w1(0, 0)
        w2_s = reorder_columns("w2_s", w2_s_raw, U8)
        for entry in (0, HALF_LIST):
            gather("v_s", U8, tab_s[:], entry, HALF_LIST)
        quantize_w1(1, 0)
        w2_w[0] = reorder_columns("w2_w0", w2_raw[0], I32)
        gather_words(1, 0, CHUNK)
        gather_words(1, CHUNK, CHUNK)
        gather_words(1, HALF_LIST, HALF_LIST)

        biased = {}
        features = {}

        def motor_pass(dst, b, t, entry, count, stop):
            half, lo = divmod(entry, HALF_LIST)
            cols = slice(P * t, P * (t + 1))
            mx_pass(dst, w2_w[b][:, cols], w2_s[4 * b : P, cols], xs_w[half][:, lo : lo + count], xs_s[:, entry : entry + count], True, stop)

        def soil_pass(dst, b, t, a, chunk, start):
            cols = slice(P * t, P * (t + 1))
            words, scales = picked["v_w%d" % a, chunk], picked["v_s", chunk][4 * a : P, :]
            mx_pass(dst, w1_w[a, b][:, cols], w1_s[a, b][:, cols], words, scales, start, a == 1)

        def add_bias(b, chunk, t, sums):
            nc.scalar.activation(biased[b, chunk][:, t, :], sums, ACT.Identity, bias=bias[:, b, t : t + 1], scale=-1.0)

        def first_soil_rows():
            biased[0, 0] = held("biased0_0", [P, PACK, CHUNK], F32)
            banks = [psum.tile([P, CHUNK], F32, name="first_bank", tag="y_bank", bufs=Y_BANKS) for t in range(Y_BANKS)]
            banks.append(psum.tile([P, CHUNK], F32, name="first_bank", tag="soil_bank", bufs=SOIL_BANKS))
            for a in range(2):
                for t in range(PACK):
                    soil_pass(banks[t][:], 0, t, a, 0, a == 0)
            for t in range(PACK):
                add_bias(0, 0, t, banks[t][:])

        def biased_rows(b, chunk, kind):
            biased[b, chunk] = held("biased%d_%d" % (b, chunk), [P, PACK, CHUNK], F32)
            with_motor = kind == "gap"
            for t0 in range(0, PACK, BANK // CHUNK):
                bank = psum.tile([P, BANK // CHUNK, CHUNK], F32, name="soil_bank", tag="soil_bank", bufs=SOIL_BANKS)
                for u in range(BANK // CHUNK):
                    if with_motor:
                        motor_pass(bank[:, u, :], b, t0 + u, chunk, CHUNK, False)
                    for a in range(2):
                        soil_pass(bank[:, u, :], b, t0 + u, a, chunk, a == 0 and not with_motor)
                for u in range(BANK // CHUNK):
                    add_bias(b, chunk, t0 + u, bank[:, u, :])

        def motor_bank(b, entry):
            bank = psum.tile([P, PACK, P], F32, name="motor_bank", tag="motor_bank", bufs=MOTOR_BANKS)
            for t in range(PACK):
                motor_pass(bank[:, t, :], b, t, entry, P, True)
            return bank

        def feature_tile(kinds, count):
            return ring.tile([P, len(kinds), count, PACK], BF16, name="feature", tag="feature", bufs=FEATURE_BUFS, align_bytes=64)

        def biased_part(b, entry, count):
            chunk, lo = entry - entry % CHUNK, entry % CHUNK
            return biased[b, chunk][:, :, lo : lo + count]

        def by_lines(planar):
            return planar.rearrange("p t (c i) -> p c t i", i=LINE)

        def by_lines_interleaved(words):
            return words.rearrange("p (c i) t -> p c t i", i=LINE)

        def quantize_features(values, b, entry, kinds):
            count = values.shape[2]
            name = "%d_%d_%d" % (kinds[0], b, entry)
            words = held("feature_w" + name, [P, len(kinds), count], U32)
            scales = held("feature_s" + name, [P, len(kinds), count], U8)
            nc.vector.quantize_mx(
                out=words[:].rearrange("p w c -> p (w c)").bitcast(FP8X4),
                scales=scales[:].rearrange("p w c -> p (w c)"),
                in_=values[:].rearrange("p w c t -> p (w c t)"),
            )
            for w, kind in enumerate(kinds):
                for c in range(0, count, P):
                    features[kind, b, entry + c] = (words[:, w, c:count], scales[:, w, c:count])

        def features_from_soil(b, entry, count, kinds):
            values = feature_tile(kinds, count)
            for c in range(0, count, P):
                motor = motor_bank(b, entry + c)
                for w, kind in enumerate(kinds):
                    nc.vector.tensor_tensor(
                        by_lines_interleaved(values[:, w, c : c + P, :]),
                        by_lines(biased_part(b, entry + c, P)),
                        by_lines(motor[:]),
                        ALU.subtract if kind == GAP else ALU.max,
                    )
            quantize_features(values, b, entry, kinds)

        def gap_from_gap_rows(b, chunk):
            values = feature_tile([GAP], CHUNK)
            nc.scalar.copy(by_lines_interleaved(values[:, 0, :, :]), by_lines(biased[b, chunk][:]))
            quantize_features(values, b, chunk, [GAP])

        def top_from_gap_rows(b, entry, count):
            values = feature_tile([TOP], count)
            for c in range(0, count, P):
                nc.vector.scalar_tensor_tensor(
                    values[:, 0, c : c + P, :],
                    biased_part(b, entry + c, P).rearrange("p t c -> p c t"),
                    0.0,
                    motor_bank(b, entry + c)[:].rearrange("p t c -> p c t"),
                    ALU.max,
                    ALU.add,
                )
            quantize_features(values, b, entry, [TOP])

        out_view = out.rearrange("(n p) s -> p n s", p=P)
        versine = {}

        def y_banks(count):
            per_bank = min(BANK // count, N_TILES)
            groups = []
            for n0 in range(0, N_TILES, per_bank):
                bank = psum.tile([P, per_bank, count], F32, name="y_bank", tag="y_bank", bufs=Y_BANKS)
                groups.append((bank, n0, min(per_bank, N_TILES - n0)))
            return groups

        def versine_rows(chunk):
            groups = y_banks(CHUNK)
            for bank, n0, tiles in groups:
                for n in range(n0, n0 + tiles):
                    for c in range(0, CHUNK, P):
                        for b in range(2):
                            words, scales = features[GAP, b, chunk + c]
                            mx_pass(
                                bank[:, n - n0, c : c + P],
                                w4_w[:, b, 2 * P * n : 2 * P * (n + 1)],
                                w4_s[:, b, P * n : P * (n + 1)],
                                words[:, 0:P],
                                scales[:, 0:P],
                                b == 0,
                                b == 1,
                                FP4X4,
                            )
            bounded = ring.tile([P, N_TILES, CHUNK], F32, name="bounded", tag="bounded")
            half_sin = ring.tile([P, N_TILES, CHUNK], F32, name="half_sin", tag="half_sin")
            versine[chunk] = held("versine%d" % chunk, [P, N_TILES, CHUNK], F32)
            for bank, n0, tiles in groups:
                nc.scalar.activation(bounded[:, n0 : n0 + tiles, :], bank[:, 0:tiles, :], ACT.Tanh)
            for n in range(N_TILES):
                nc.scalar.activation(half_sin[:, n, :], bounded[:, n, :], ACT.Sin, bias=zero[:], scale=half_swing[:, n : n + 1])
            for tiles in (slice(0, 1), slice(1, N_TILES)):
                nc.scalar.activation(versine[chunk][:, tiles, :], half_sin[:, tiles, :], ACT.Square, scale=math.sqrt(2.0))

        def finish(entry, count):
            chunk, lo = entry - entry % CHUNK, entry % CHUNK
            groups = y_banks(count)
            for bank, n0, tiles in groups:
                for n in range(n0, n0 + tiles):
                    for b in range(2):
                        words, scales = features[TOP, b, entry]
                        cols = slice(N * b + P * n, N * b + P * (n + 1))
                        mx_pass(bank[:, n - n0, :], w3_w[:, cols], w3_s[:, cols], words[:, 0:count], scales[:, 0:count], b == 0, b == 1)
            result = held("result%d" % entry, [P, N_TILES, count], F32)
            for bank, n0, tiles in groups:
                rows = slice(n0, n0 + tiles)
                nc.vector.scalar_tensor_tensor(
                    result[:, rows, :], versine[chunk][:, rows, lo : lo + count], -1.0, bank[:, 0:tiles, :], ALU.add, ALU.add
                )
                nc.sync.dma_start(out_view[:, rows, entry : entry + count], result[:, rows, :])

        c0, c1, c2, c3 = range(0, S, CHUNK)
        both = [GAP, TOP]

        first_soil_rows()
        w2_w[1] = reorder_columns("w2_w1", w2_raw[1], I32)
        features_from_soil(0, c0, CHUNK, both)
        biased_rows(0, c1, "soil")
        round_w1(0, 1)
        biased_rows(0, c2, "soil")
        round_w1(1, 1)
        quantize_w1(0, 1)
        features_from_soil(0, c1, CHUNK, both)
        quantize_w1(1, 1)
        round_w3()
        features_from_soil(0, c2, CHUNK, both)

        biased_rows(0, c3, "gap")
        biased_rows(1, c0, "soil")
        gap_from_gap_rows(0, c3)
        top_from_gap_rows(0, c3, P)

        features_from_soil(1, c0, CHUNK, both)
        biased_rows(1, c1, "soil")
        features_from_soil(1, c1, CHUNK, both)
        biased_rows(1, c2, "gap")
        gap_from_gap_rows(1, c2)
        biased_rows(1, c3, "soil")
        versine_rows(c0)
        quantize_w3()
        features_from_soil(1, c3, CHUNK, [GAP])

        versine_rows(c1)
        finish(c0, CHUNK)
        versine_rows(c2)
        top_from_gap_rows(1, c2, CHUNK)
        finish(c1, CHUNK)
        versine_rows(c3)
        top_from_gap_rows(0, c3 + P, P)
        for entry in (c3, c3 + P):
            features_from_soil(1, entry, P, [TOP])
        finish(c2, CHUNK)
        for entry in (c3, c3 + P):
            finish(entry, P)
